import numpy as np, ml_dtypes
CORES = [113,118,241,246]
N = 4
BF = ml_dtypes.bfloat16
V, C, S, IT, Q, RO, D = 1536, 256, 256, 5, 11, 2, 2048
P = V + 2 * C * RO
def mesh(rng, m, isb, chain):
    o = rng.permutation(V); x = np.zeros(3 * V, np.int64); sn = np.zeros(2 * S, np.int64); rest = V - 2 * m
    x[2 * V + o[0:2 * m:2]] = o[1:2 * m:2]; x[2 * V + o[1:2 * m:2]] = o[0:2 * m:2]
    up = 2 * V + o[2 * m:]; leg = rng.integers(0, 2, rest) * V + o[:rest] if chain else rng.permutation(2 * V)[:rest]
    left = np.ones(2 * V, bool); left[leg] = False
    jb, jl = np.flatnonzero(isb), np.flatnonzero(~isb); c = rng.permutation(rest); cut, keep = c[:len(jb)], c[len(jb):]
    x[up[keep]] = leg[keep] % V; x[leg[keep]] = up[keep] - 2 * V
    x[up[cut]] = P + jb; sn[jb] = up[cut] - 2 * V
    pool = np.concatenate([rng.permutation(leg[cut]), rng.permutation(np.flatnonzero(left))]); h = rng.permutation(pool[:len(jl)])
    x[h] = P + jl; sn[jl] = h % V
    k = rng.permutation(pool[len(jl):]).reshape(2, -1); x[k[0]] = k[1] % V; x[k[1]] = k[0] % V
    return x.reshape(3, V), sn, o
def meshes(rng, m, chain=False):
    x = rng.choice(4, (N, 8, S), p=[0.35, 0.35, 0.2, 0.1])
    isb = np.concatenate([np.roll((x == 1) | (x == 3), 1, axis=0), (x == 0) | (x == 3)], axis=2)
    z = [[mesh(rng, int(m[a, g]), isb[a, g], chain) for g in range(8)] for a in range(N)]
    return tuple(np.stack([np.stack([u[i] for u in row]) for row in z]) for i in range(3))
def levels(rng):
    return rng.permuted(np.tile(np.array([60, 90, 110, 130, 150, 165, 180, 200]), (N, 1)), axis=1)[:, :, None, None] + rng.integers(-20, 21, (N, 8, 16, 1))
def errors(rng):
    return (256 * (0.25 + 0.75 * rng.random((N, 8, 1, V))) * rng.random((N, 8, 16, V))).astype(np.int64)
def under(rng, th):
    return np.minimum((th * rng.random((N, 8, 16, V))).astype(np.int64), th - 1)
def plant(rng, e, t, x, y, cnt):
    on = np.argsort(rng.random((16, len(x))), axis=0) < cnt[None, :]; one = rng.random(on.shape) < 0.5
    v = np.where(rng.random(on.shape) < 0.5, t, np.minimum(t + (rng.random(on.shape) * (256 - t)).astype(np.int64), 255))
    e[:, x] = np.where(on & one, v, e[:, x]); e[:, y] = np.where(on & ~one, v, e[:, y])
def more(rng):
    return rng.integers(0, 256, (N, 8, 16, D)), rng.integers(0, 256, (N, 8, 16, 1))
def pack(err, p, sn, det, wt, th):
    b = lambda a: np.ascontiguousarray(a.reshape(N, 128, -1)).astype(np.float32).astype(BF)
    i = lambda a: np.ascontiguousarray(a).astype(np.int32)
    return {"err": b(err), "lt": i(p[:, :, 0]), "rt": i(p[:, :, 1]), "bs": i(p[:, :, 2]), "snd": i(sn), "det": b(det), "wt": i(wt.reshape(N, 128, 1)), "th": i(th.reshape(N, 128, 1))}
def setup_inputs(rng):
    p, sn, o = meshes(rng, rng.integers(V // 8, V // 3 + 1, (N, 8))); det, wt = more(rng)
    return pack(errors(rng), p, sn, det, wt, levels(rng))
def setup_inputs_room(rng):
    M = V // 3; p, sn, o = meshes(rng, np.full((N, 8), M)); det, wt = more(rng)
    th = np.repeat(rng.integers(64, 192, (1, 8, 16, 1)), N, axis=0); err = under(rng, th)
    for a in range(N):
        for g in range(8):
            n = (C, C + 1, 0, 1, C - 1, M, C, C + 1)[(a + g) % 8]
            plant(rng, err[a, g], th[a, g], o[a, g, 0:2 * M:2], o[a, g, 1:2 * M:2], np.where(rng.permutation(M) < n, Q, Q - 1))
    return pack(err, p, sn, det, wt, th)
def setup_inputs_chain(rng):
    M = V // (2 * (IT + 3)); p, sn, o = meshes(rng, np.full((N, 8), M), True); det, wt = more(rng)
    th = np.repeat(rng.integers(64, 192, (1, 8, 16, 1)), N, axis=0); err = under(rng, th); far = np.array([0, 1, IT - 1, IT, IT, IT + 1, IT + 1])
    for a in range(N):
        for g in range(8):
            i = 2 * np.arange(M) + 2 * M * rng.permuted(np.resize(far, M))
            plant(rng, err[a, g], th[a, g], o[a, g, i], o[a, g, i + 1], np.where(rng.random(M) < 0.8, Q, Q - 1))
    return pack(err, p, sn, det, wt, th)
def setup_inputs_ties(rng):
    p, sn, o = meshes(rng, rng.integers(V // 8, V // 3 + 1, (N, 8))); det, wt = more(rng)
    th = np.clip(np.array([1, 2, 100, 128, 254, 255, 255, 30])[None, :, None, None] + rng.integers(-1, 2, (N, 8, 16, 1)), 1, 255); th[:, 6] = 255
    err = np.clip(th - 1 + (rng.random((N, 8, 16, V)) < 0.5 * rng.random((N, 8, 1, V))) * rng.integers(1, 3, (N, 8, 16, V)), 0, 255)
    err[:, 6] = np.minimum(err[:, 6], 254); err[:, 7] = 255
    det[:, 1] = 255; det[:, 2] = 0; wt[:, 0] = 0; wt[:, 1] = 255
    return pack(err, p, sn, det, wt, th)
def pools(rng):
    return [[int(z) for z in rng.permutation(V)] for a in range(N)], rng.permutation(S)[:8 * N].reshape(N, 2, 4)
def watch(x, leg, u, v, slot):
    x[leg, u] = P + slot; x[1 - leg, u] = v; x[2, u] = v; x[:, v] = u
def renamed(rng, x, sn, e):
    pool, kk = pools(rng)
    for a in range(N):
        for s in range(2):
            k, k2, kb, kb2 = [int(z) for z in kk[a, s]]; q, z = (a + 2 * s - 1) % N, (a - 2 * s + 1) % N
            t, b = pool[a].pop(), pool[a].pop()
            x[a, 2, t] = b; x[a, 2, b] = t; x[a, 0, t] = P + (1 - s) * S + k2; x[a, 1, t] = P + s * S + k; e[a, :, t] = 255
            sn[a, s * S + k] = t; sn[a, (1 - s) * S + k] = t
            u, v = pool[q].pop(), pool[q].pop(); sn[q, (1 - s) * S + k] = u; watch(x[q], s, u, v, (1 - s) * S + k)
            u, v = pool[z].pop(), pool[z].pop(); sn[z, s * S + k2] = u; watch(x[z], 1 - s, u, v, s * S + k)
            t, b = pool[a].pop(), pool[a].pop()
            x[a, 2, t] = b; x[a, 2, b] = t; x[a, 0, t] = P + s * S + kb2; e[a, :, t] = 255
            x[a, 1, t] = (P + s * S + kb) % (2 * S) + 2 * S * int(rng.integers(0, V // (2 * S))); sn[a, s * S + kb] = t
            u, v = pool[q].pop(), pool[q].pop(); sn[q, (1 - s) * S + kb2] = u; watch(x[q], s, u, v, (1 - s) * S + kb)
def allpairs(rng, x, e):
    for a in range(N):
        pr = np.sort(rng.permutation(V).reshape(-1, 2), axis=1); pr = pr[np.argsort(pr[:, 0])]
        x[a, 0, pr[0::2]] = pr[1::2]; x[a, 0, pr[1::2]] = pr[0::2]
        for i in (1, 2):
            x[a, i, pr[:, 0]] = pr[:, 1]; x[a, i, pr[:, 1]] = pr[:, 0]
        e[a][:, pr[len(pr) - C // 2:].reshape(-1)] = 255
def crowded(rng, x, sn, e):
    pool, kk = pools(rng)
    for a in range(N):
        for s in range(2):
            q = (a + 2 * s - 1) % N
            for i in range(2):
                k, kn = int(kk[a, s, 2 * i]), int(kk[a, s, 2 * i + 1]); many = [pool[a].pop() for z in range(V // 16)]
                x[a, 2, np.array(many)] = P + s * S + kn
                t = max(many) if i == 0 else min(many); e[a, :, t] = 255; sn[a, s * S + k] = t
                u, v = pool[q].pop(), pool[q].pop(); sn[q, (1 - s) * S + kn] = u; watch(x[q], 1 - i, u, v, (1 - s) * S + k)
def newbases(rng, x, sn, e, th):
    pool, kk = pools(rng)
    for a in range(N):
        pr = np.sort(np.array(pool[a][:2 * S]).reshape(S, 2), axis=1); pr = pr[np.argsort(pr[:, 0])]
        x[a, 2, pr[:, 0]] = pr[:, 1]; x[a, 2, pr[:, 1]] = pr[:, 0]
        plant(rng, e[a], th[a], pr[:, 0], pr[:, 1], rng.integers(Q, 17, S))
        for s in range(2):
            q = (a + 2 * s - 1) % N
            for i in range(2):
                k, kn = int(kk[a, s, 2 * i]), int(kk[a, s, 2 * i + 1]); j = (s * S + kn + P - V) % (2 * S)
                y = int(pr[j // 2, j % 2]); w = pool[a].pop()
                x[a, :, w] = y; x[a, 1, y] = w; e[a, :, w] = 255; sn[a, s * S + k] = w
                u, v = pool[q].pop(), pool[q].pop(); sn[q, (1 - s) * S + kn] = u; watch(x[q], i, u, v, (1 - s) * S + k)
def setup_inputs_free(rng):
    p = rng.choice(np.concatenate([np.arange(V), P + np.arange(2 * S)]), (N, 8, 3, V)); sn = rng.integers(0, V, (N, 8, 2 * S)); m = V // 4
    det, wt = more(rng); err = errors(rng); th = levels(rng)
    for a in range(N):
        for g in range(0, 8, 2):
            o = rng.permutation(V); x = p[a, g]; x[2, o[0:2 * m:2]] = o[1:2 * m:2]; x[2, o[1:2 * m:2]] = o[0:2 * m:2]
            v = o[2 * m:]; v = v[x[2, v] < V]; x[rng.integers(0, 2, len(v)), x[2, v]] = v
            x[0, o[:40]] = o[:40]; x[1, o[20:60]] = o[20:60]; x[0, o[100:140]] = x[1, o[100:140]]; x[1, o[200:240:2]] = o[201:240:2]
            j = rng.permutation(2 * S)[:S // 2]; x[1, sn[a, g, j]] = P + j
    for a in range(N):
        for g in range(0, 8, 2):
            for s in range(2):
                q = (a + 2 * s - 1) % N; k = rng.integers(0, S, 32); k2 = rng.integers(0, S, 32)
                p[q, g, 2, sn[q, g, (1 - s) * S + k]] = P + (1 - s) * S + k2
                p[a, g, rng.integers(0, 2, 32), sn[a, g, s * S + k2]] = P + s * S + k
    p[:, 0, 2, 0] = V - 1; p[:, 0, 2, V - 1] = 0; err[:, 0, :, 0] = 255; err[:, 0, :, V - 1] = 255
    n = 16; me = np.arange(V); two, lone = {}, {}
    for a in range(N):
        for g in range(0, 8, 2):
            x = p[a, g]
            b = np.minimum(x[2], V - 1); pair = (x[2] < V) & (x[2, b] == me) & (b != me)
            t = rng.permutation(np.flatnonzero(pair & (me < b) & (me > 0)))
            two[a, g] = rng.permuted(np.stack([t[:2 * n], b[t[:2 * n]]]), axis=0)
            lone[a, g] = rng.permutation(np.flatnonzero(~pair & (me > 0) & (me < V - 1)))[:2 * n]
            cut = t[C - 4 * n:]; x[2, cut] = P + rng.integers(0, 2 * S, len(cut))
    for g in range(0, 8, 2):
        k, k2 = rng.permutation(S)[:2 * n].reshape(2, n)
        for a in range(N):
            for s in range(2):
                q = (a + 2 * s - 1) % N; u, v = two[a, g][:, s * n:(s + 1) * n]; w = lone[q, g][(1 - s) * n:(2 - s) * n]
                sn[a, g, s * S + k2] = u; sn[q, g, (1 - s) * S + k] = w
                x = p[a, g]; x[0, u] = P + s * S + k; x[1, u] = v; x[0, v] = u; x[1, v] = u
                p[q, g, 2, w] = np.where(np.arange(n) < n // 2, P + s * S + k2, (P + k2) % S + S * rng.integers(0, V // S, n))
                e = err[a, g]; c = np.concatenate([u, v]); e[:, c] = np.minimum(e[:, c], th[a, g] - 1)
                plant(rng, err[q, g], th[a, g], w, w, rng.integers(Q, 17, n))
    th[:, 1::2] = rng.integers(20, 121, (N, 4, 16, 1)); err[:, 1::2] = under(rng, th)[:, 1::2]
    p[:, 1::2, 2] = P + rng.integers(0, 2 * S, (N, 4, V)); p[:, 5] = P + rng.integers(0, 2 * S, (N, 3, V))
    sn[:, 5] = rng.choice(np.array([0, V - 1, V // 2, 5]), (N, 2 * S))
    renamed(rng, p[:, 1], sn[:, 1], err[:, 1]); allpairs(rng, p[:, 3], err[:, 3])
    crowded(rng, p[:, 5], sn[:, 5], err[:, 5]); newbases(rng, p[:, 7], sn[:, 7], err[:, 7], th[:, 7])
    return pack(err, p, sn, det, wt, th)
def setup_inputs_spread(rng):
    p, sn, o = meshes(rng, rng.integers(V // 8, V // 3 + 1, (N, 8)))
    err = (np.exp2(8 * rng.random((N, 8, 1, V))) * rng.random((N, 8, 16, V))).astype(np.int64)
    det = (np.exp2(8 * rng.random((N, 8, 1, D))) * rng.random((N, 8, 16, D))).astype(np.int64)
    wt = np.minimum(np.exp2(8 * rng.random((N, 8, 16, 1))).astype(np.int64), 255)
    th = np.clip(np.exp2(3 + 5 * rng.random((N, 8, 1, 1)) + rng.random((N, 8, 16, 1)) - 0.5).astype(np.int64), 1, 255)
    return pack(np.minimum(err, 255), p, sn, np.minimum(det, 255), wt, th)
def check_inputs(d):
    bad = []
    for k in ("err", "det"):
        x = np.asarray(d[k]).astype(np.float32)
        if not np.all((x >= 0) & (x <= 255) & (x == np.floor(x))): bad.append("range of " + k)
    for k in ("lt", "rt", "bs"):
        x = d[k]
        if not np.all(((x >= 0) & (x < V)) | ((x >= P) & (x < P + 2 * S))): bad.append("range of " + k)
    for k, lo, hi in (("snd", 0, V - 1), ("wt", 0, 255), ("th", 1, 255)):
        if np.min(d[k]) < lo or np.max(d[k]) > hi: bad.append("range of " + k)
    return bad
def ghosts(x):
    return np.concatenate([np.roll(x[..., S:], 1, axis=0), np.roll(x[..., :S], -1, axis=0)], axis=-1)
def reference(err, lt, rt, bs, snd, det, wt, th):
    take = np.take_along_axis; me = np.arange(P)
    e = np.zeros((N, 8, 16, P), np.int32); e[..., :V] = err.astype(np.float32).astype(np.int32).reshape(N, 8, 16, V)
    dt = det.astype(np.float32).astype(np.int32).reshape(N, 8, 16, D); wq = wt.astype(np.int32).reshape(N, 8, 16, 1); tq = th.astype(np.int32).reshape(N, 8, 16, 1)
    p = np.zeros((N, 8, 3, P), np.int64) + me
    p[:, :, 0, :V] = lt; p[:, :, 1, :V] = rt; p[:, :, 2, :V] = bs
    sn = snd.astype(np.int64)
    lo = np.repeat(np.array([0, S]), S); off = np.repeat(np.array([-S, S]), S)
    for t in range(RO):
        L, R, B = p[:, :, 0], p[:, :, 1], p[:, :, 2]
        j = ghosts(take(B, sn, 2)) - P + off
        gb = np.where((j >= lo) & (j < lo + S), take(sn, np.clip(j, 0, 2 * S - 1), 2), -1)
        base = np.concatenate([B, gb], axis=2); gl = (take(base, L, 2) == me)[:, :, None]; gr = (take(base, R, 2) == me)[:, :, None]
        W = e
        for it in range(IT):
            A = np.concatenate([W, ghosts(take(W, sn[:, :, None], 3))], axis=3)
            W = np.maximum(W, np.maximum(np.where(gl, take(A, L[:, :, None], 3), 0), np.where(gr, take(A, R[:, :, None], 3), 0)))
        bo = np.minimum(B, P - 1); pair = (B < P) & (take(B, bo, 2) == me) & (me < B)
        rows = np.add.reduce((np.maximum(W, take(W, bo[:, :, None], 3)) >= tq).astype(np.int32), axis=2)
        go = (pair & (rows >= Q)).astype(np.int64); k = np.add.accumulate(go, axis=2) - go
        a, g, x = np.nonzero((go == 1) & (k < C)); y = B[a, g, x]
        new = np.zeros((N, 8, P), np.int64)
        new[a, g, x] = V + 2 * C * t + 2 * k[a, g, x]; new[a, g, y] = new[a, g, x] + 1
        nx = np.concatenate([new, np.zeros((N, 8, 2 * S), np.int64)], axis=2); rx = np.concatenate([R, np.full((N, 8, 2 * S), -1)], axis=2)
        pn = np.stack([np.where((take(nx, T, 2) > 0) & (take(rx, T, 2) == me), take(nx, T, 2), T) for T in (L, R, B)], axis=2)
        sn = np.where((take(new, sn, 2) > 0) & (take(R, sn, 2) == P + np.arange(2 * S)), take(new, sn, 2), sn)
        a = np.concatenate([a, a]); g = np.concatenate([g, g]); s = np.concatenate([x, y]); o = np.concatenate([y, x])
        n, m = new[a, g, s], new[a, g, o]; bl, br = pn[a, g, 0, s], pn[a, g, 1, s]
        pn[a, g, 0, s] = n; pn[a, g, 1, s] = m; pn[a, g, 2, s] = bl
        pn[a, g, 0, n] = o; pn[a, g, 1, n] = s; pn[a, g, 2, n] = br
        p = pn
        es = e[a, g, :, s]; h = np.add.reduce(wq * e, axis=2)[a, g, s]
        for place in (s, n):
            e[a, g, :, place] = (es >> 1) + (dt[a, g, :, (h + place) & (D - 1)] >> 1)
    return {"ye": e.reshape(N, 128, P).astype(np.float32).astype(BF), "yl": p[:, :, 0].astype(np.float32), "yr": p[:, :, 1].astype(np.float32), "yb": p[:, :, 2].astype(np.float32)}

@@ -1,0 +1,700 @@
+import numpy as np
+from concourse.mybir import dt, AluOpType, AxisListType, ActivationFunctionType
+
+OP = AluOpType
+AF = ActivationFunctionType
+NR = 4
+V0 = 1536
+GH = 2560
+OWN = 528
+
+SCRATCH = {}
+PK = {}
+
+
+def _pack(big, dtype, parts):
+    o = 0
+    for n, c in parts:
+        PK[n] = (big, o)
+        o += (c + 15) // 16 * 16
+    SCRATCH[big] = ("sbuf", [128, o], dtype)
+
+
+_pack("kf", "float32", (("pq", 16), ("meS", 160), ("slotc", 32), ("zer", 128), ("thf", 1), ("wtf", 1), ("ab", 2),
+                        ("st0", 352), ("st1", 448), ("ns0", 288), ("ns1", 384), ("ns2", 480), ("sn0", 32), ("sn1", 32),
+                        ("ixa", 320), ("ixb", 320), ("ulf", 320), ("mB", 128), ("mB2", 128), ("pe", 128), ("thr", 128),
+                        ("xo", 32), ("xz", 32), ("xo2", 32), ("sc", 128), ("ka", 128), ("kc", 128), ("kd", 128),
+                        ("pm2", 384), ("fl", 384), ("lff", 384), ("t32", 32), ("z", 512), ("pt", 384), ("q3", 384),
+                        ("q3u", 384), ("sp", 128), ("nsp", 128), ("ysn", 256), ("yss", 256), ("oa", 128), ("ob", 128),
+                        ("oc", 128), ("od", 128), ("tsw", 32), ("tab", 32), ("td", 32), ("zy", 32), ("yzy", 32), ("yt", 32),
+                        ("yu", 32), ("snv", 32), ("sna", 32), ("snb", 32), ("snc", 32), ("hq", 64), ("hm", 64), ("pres", 64)))
+_pack("ki", "int32", (("nraw", 288), ("nsn", 32), ("thi", 1), ("wti", 1), ("ik", 16), ("ik2", 16), ("pmi", 160), ("pmod", 160),
+                      ("c16", 160), ("hz", 64), ("hz2", 64)))
+_pack("ku", "uint16", (("li0", 352), ("li1", 448), ("snl0", 32), ("snl1", 32), ("gbo", 32), ("bo", 32), ("ul", 320), ("pl", 128),
+                       ("koff", 128), ("tl", 16), ("TL", 32), ("lf", 384), ("snf", 32), ("eo", 64)))
+_pack("kh", "float16", (("n16", 288), ("nsn16", 32), ("ra", 1536), ("rb", 1536), ("rc", 1536), ("bs16", 512), ("ls16", 1024),
+                        ("T16", 512), ("Y16", 512), ("x16", 384), ("sn16", 32), ("me16", 128)))
+_pack("kb", "bfloat16", (("ones", 128), ("eye", 128), ("blk", 128), ("blka", 128), ("tri", 128), ("ltg", 128), ("jq", 256),
+                         ("jrow", 512), ("go", 128), ("eT", 512), ("e2", 512), ("e2b", 512), ("cT", 512), ("vs", 512), ("vy", 512),
+                         ("sb0", 512), ("sb1", 512), ("sb2", 512), ("sb3", 512), ("sb4", 512)))
+for _n, _c, _d in (("brow", 3088, "float32"), ("lrow", 3088, "float32"), ("rrow", 3088, "float32"), ("mex", 2560, "float32"),
+                   ("snt", 544, "float32"), ("fr", 2048, "float32"), ("MDf", 2048, "float32"),
+                   ("MD", 2048, "bfloat16"), ("EQ", 2048, "bfloat16"), ("CQ", 2048, "bfloat16"), ("WQ", 2048, "bfloat16"),
+                   ("dtb", 2064, "bfloat16"), ("NT", 2576, "bfloat16"), ("vL", 2048, "bfloat16"), ("vR", 2560, "bfloat16"),
+                   ("vB", 2048, "bfloat16"), ("U0", OWN + 2560, "bfloat16"), ("U1", OWN + 2048, "bfloat16"),
+                   ("U2", OWN + 2048, "bfloat16"), ("U3", OWN + 2048, "bfloat16"), ("U4", OWN + 2048, "bfloat16"),
+                   ("u5", 2048, "bfloat16"), ("gr0", 2560, "bfloat16"), ("gr1", 2560, "bfloat16"), ("in0", 2048, "bfloat16"),
+                   ("in1", 2048, "bfloat16")):
+    SCRATCH[_n] = ("sbuf", [128, _c], _d)
+for _n in range(8):
+    SCRATCH["p%d" % _n] = ("psum", [128, 512], "float32")
+
+KINDS = ["b", "0", "1", "2", "3", "4"]
+SEMAPHORES = (["cv", "cs", "cp", "cg"] + ["d%d" % i for i in range(24)]
+              + ["r%s%d" % (k, s) for k in KINDS for s in range(2)] + ["l%s%d" % (k, s) for k in KINDS for s in range(2)])
+
+
+def _is_psum(n):
+    return len(n) == 2 and n[0] == "p" and n[1].isdigit()
+
+
+def rank_program(g, core, T, topo):
+    rank = T.rank_of(core)
+    if rank is None:
+        return
+    nb_core = [T.cores[(rank - 1) % NR], T.cores[(rank + 1) % NR]]
+    order = sorted(range(2), key=lambda s: nb_core[s] in topo.cores_of(core))
+
+    Q = {"V": g.vector, "S": g.scalar, "P": g.tensor, "G": g, "Y": g.sync}
+    SEM = {"V": "cv", "S": "cs", "P": "cp", "G": "cg"}
+    cnt = {}
+    known = {q: {} for q in Q}
+    snaps = {}
+    hist = {}
+
+    def wait_for(q, need):
+        for s in sorted(need):
+            v = need[s]
+            if known[q].get(s, 0) >= v:
+                continue
+            Q[q].wait_ge(T.sem[s], v)
+            known[q][s] = v
+            for s2, v2 in snaps.get((s, v), {}).items():
+                if known[q].get(s2, 0) < v2:
+                    known[q][s2] = v2
+
+    def needs(q, reads, writes):
+        need = {}
+        for regs, w in ((reads, 0), (writes, 1)):
+            for n, lo, hi in regs:
+                ps = _is_psum(n)
+                for e in hist.get(n, []):
+                    if not ps and (e[0] >= hi or lo >= e[1]):
+                        continue
+                    if ps:
+                        if e[5] == q and (q == "P" or not (w or e[2])):
+                            continue
+                    elif not (w or e[2]):
+                        continue
+                    if need.get(e[3], 0) < e[4]:
+                        need[e[3]] = e[4]
+        return need
+
+    def note(q, reads, writes, sem, val):
+        snaps[(sem, val)] = dict(known[q]) if q else {}
+        for regs, w in ((writes, 1), (reads, 0)):
+            for n, lo, hi in regs:
+                old = hist.get(n, [])
+                if w:
+                    old = [e for e in old if not (lo <= e[0] and e[1] <= hi)]
+                else:
+                    old = [e for e in old if not (e[2] == 0 and e[3] == sem and lo <= e[0] and e[1] <= hi)]
+                old.append((lo, hi, w, sem, val, q))
+                hist[n] = old
+
+    def op(q, fns, reads, writes):
+        wait_for(q, needs(q, reads, writes))
+        s = SEM[q]
+        for f in fns:
+            f().then_inc(T.sem[s], 1)
+            cnt[s] = cnt.get(s, 0) + 1
+        note(q, reads, writes, s, cnt[s])
+
+    ndma = [0]
+
+    def dma(q, out, in_):
+        wait_for(q, needs(q, in_[1], out[1]))
+        s = "d%d" % ndma[0]
+        ndma[0] += 1
+        Q[q].dma_start(out[0], in_[0]).then_inc(T.sem[s], 16)
+        cnt[s] = 16
+        note(q, in_[1], out[1], s, 16)
+
+    def X(n, lo, hi, st=1):
+        if n in PK:
+            t, o = T[PK[n][0]], PK[n][1]
+        else:
+            t, o = T[n], 0
+        return t[:, o + lo:o + hi] if st == 1 else t[:, o + lo:o + hi:st]
+
+    def A(n, lo, hi, st=1):
+        return (X(n, lo, hi, st), [(n, lo, hi)])
+
+    def ind(w, o):
+        return (w[0].indirect(o[0]), w[1] + o[1])
+
+    def tt(out, a, b, f):
+        op("V", [lambda: g.vector.tensor_tensor(out[0], a[0], b[0], f)], a[1] + b[1], out[1])
+
+    def ts(out, a, s1, f1, s2=None, f2=None):
+        r = list(a[1])
+        v1 = s1
+        if isinstance(s1, tuple):
+            r += s1[1]
+            v1 = s1[0]
+        if f2 is None:
+            op("V", [lambda: g.vector.tensor_scalar(out[0], a[0], v1, None, f1)], r, out[1])
+        else:
+            op("V", [lambda: g.vector.tensor_scalar(out[0], a[0], v1, s2, f1, f2)], r, out[1])
+
+    def cp(out, a):
+        op("V", [lambda: g.vector.tensor_copy(out[0], a[0])], a[1], out[1])
+
+    def scat(w, o, a):
+        op("V", [lambda: g.vector.tensor_copy(w[0].indirect(o[0]), a[0])], a[1] + o[1], w[1])
+
+    def ms(out, v):
+        op("V", [lambda: g.vector.memset(out[0], v)], [], out[1])
+
+    def act(out, a, f=AF.Copy, bias=0.0, scale=1.0):
+        r = list(a[1])
+        sc = scale
+        if isinstance(scale, tuple):
+            r += scale[1]
+            sc = scale[0]
+        bi = bias
+        if isinstance(bias, tuple):
+            r += bias[1]
+            bi = bias[0]
+        op("S", [lambda: g.scalar.activation(out[0], a[0], f, bias=bi, scale=sc)], r, out[1])
+
+    def iota(out, pattern, base, cm, small=True):
+        if small:
+            op("G", [lambda: g.iota(out[0], pattern, base, cm, allow_small_or_imprecise_dtypes=True)], [], out[1])
+        else:
+            op("G", [lambda: g.iota(out[0], pattern, base, cm)], [], out[1])
+
+    def sel(out, a, pattern, cmp, base, cm):
+        op("G", [lambda: g.affine_select(out[0], a[0], pattern, cmp, 0.0, base, cm)], a[1], out[1])
+
+    bank = [4]
+
+    def wb():
+        b = bank[0]
+        bank[0] = 4 + (b - 3) % 4
+        return "p%d" % b
+
+    def mm(b, jobs):
+        fns, rd = [], []
+        for o, l, r, s0, s1 in jobs:
+            fns.append(lambda o=o, l=l, r=r, s0=s0, s1=s1: g.tensor.matmul(o[0], l[0], r[0], s0, s1))
+            for x in (l, r):
+                if x[1][0] not in rd:
+                    rd.append(x[1][0])
+        op("P", fns, rd, [(b, 0, 512)])
+
+    def conv(b, jobs):
+        js = []
+        for lo, hi, st, m, rh in jobs:
+            for q in range(16):
+                js.append((A(b, lo, hi, st), A(m, 128 * q, 128 * q + 128), rh(q), q == 0, q == 15))
+        mm(b, js)
+
+    def rS(n, lo, hi):
+        return lambda q: (X(n, lo + q, hi, 16), [(n, lo, hi)])
+
+    def chosen(src, dst):
+        return topo.engines(src, dst)[-8:]
+
+    def send(s, kind, src, dst, lo, hi):
+        d = nb_core[s]
+        wait_for("G", needs("G", src[1], []))
+        rid, pid = topo.addr(d, core)
+        es = chosen(core, d)
+        ls = "l%s%d" % (kind, s)
+        g.remote_dma(X(dst, lo, hi), src[0], T.sem["r%s%d" % (kind, 1 - s)], T.sem[ls], pid, rid, sum(1 << e for e in es))
+        cnt[ls] = cnt.get(ls, 0) + len(es)
+        note("G", src[1], [], ls, cnt[ls])
+
+    def recv(s, kind, dst, lo, hi):
+        rs = "r%s%d" % (kind, s)
+        cnt[rs] = cnt.get(rs, 0) + len(chosen(nb_core[s], core))
+        note(None, [], [(dst, lo, hi)], rs, cnt[rs])
+
+    def HB(n):
+        return T[n][:]
+
+    PP, NW, LW = (V0, 2048), (96, 128), (128, 160)
+
+    dma("Y", A("nsn", 0, 32), (HB("snd"), []))
+    dma("S", A("nraw", 192, 288), (HB("bs"), []))
+    dma("Y", A("nraw", 96, 192), (HB("rt"), []))
+    dma("S", A("nraw", 0, 96), (HB("lt"), []))
+    dma("Y", A("U0", OWN, OWN + V0), (HB("err"), []))
+    dma("S", A("thi", 0, 1), (HB("th"), []))
+    dma("S", A("wti", 0, 1), (HB("wt"), []))
+    dma("Y", A("dtb", 0, 2048), (HB("det"), []))
+
+    ms(A("ones", 0, 128), 1.0)
+    iota(A("ik", 0, 16), [[-1, 16]], 16, 1, False)
+    sel(A("blka", 0, 128), A("ones", 0, 128), [[-16, 8], [0, 16]], OP.is_ge, 0, 1)
+    sel(A("blk", 0, 128), A("blka", 0, 128), [[16, 8], [0, 16]], OP.is_ge, 15, -1)
+    sel(A("eye", 0, 128), A("ones", 0, 128), [[-1, 128]], OP.is_equal, 0, 1)
+    iota(A("pmi", 0, 160), [[0, 160]], 0, 1, False)
+    iota(A("c16", 0, 160), [[16, 160]], 0, 0, False)
+    iota(A("brow", V0, GH), [[2, 512], [-1, 2]], V0 + 1, 0)
+    iota(A("mex", 512, 2560), [[1, 2048]], 0, 0)
+    ts(A("ik2", 0, 16), A("ik", 0, 16), 15, OP.bitwise_and)
+    ts(A("pq", 0, 16), A("ik2", 0, 16), 0, OP.is_equal)
+    for q in range(16):
+        ts(A("EQ", 128 * q, 128 * q + 128), A("blk", 0, 128), A("pq", q, q + 1), OP.mult)
+        act(A("MD", 128 * q, 128 * q + 128), A("eye", 0, 128), AF.Copy, scale=A("pq", q, q + 1))
+    ts(A("nsn16", 0, 32), A("nsn", 0, 32), -1536, OP.add)
+    ts(A("n16", 192, 288), A("nraw", 192, 288), -1536, OP.add)
+    ts(A("n16", 0, 192), A("nraw", 0, 192), -1536, OP.add)
+
+    def nrow(x, lo, row, r16):
+        for i in range(4):
+            b = wb()
+            k = min(5, 16 - 5 * i)
+            mm(b, [(A(b, 96 * j, 96 * j + 96), A("EQ", 128 * (5 * i + j), 128 * (5 * i + j) + 128), A(x, lo, lo + 96), True, True)
+                   for j in range(k)])
+            act(A(row, 480 * i, 480 * i + 96 * k), A(b, 0, 96 * k), AF.Identity, bias=1536.0)
+            cp(A(r16, 480 * i, 480 * i + 96 * k), A(b, 0, 96 * k))
+
+    b = wb()
+    mm(b, [(A(b, 32 * q, 32 * q + 32), A("EQ", 128 * q, 128 * q + 128), A("nsn16", 0, 32), True, True) for q in range(16)])
+    cp(A("bs16", 0, 512), A(b, 0, 512))
+    sb = b
+    b = wb()
+    conv(b, [(0, 32, 1, "MD", rS("bs16", 0, 512))])
+    ts(A("snl0", 0, 32), A(b, 0, 32), 1536, OP.add)
+    ts(A("sn0", 0, 32), A(b, 0, 32), 1536, OP.add)
+    act(A("mex", 0, 512), A(sb, 0, 512), AF.Identity, bias=1536.0)
+
+    def sndtab():
+        for s in range(2):
+            act(A("snt", 272 * s, 272 * s + 256), A("mex", 256 * s, 256 * s + 256))
+
+    nrow("n16", 192, "brow", "ra")
+    nrow("n16", 96, "rrow", "rb")
+    nrow("n16", 0, "lrow", "rc")
+    sndtab()
+    ms(A("snt", 256, 272), -1.0)
+    ms(A("snt", 528, 544), -1.0)
+    for i in range(5):
+        ms(A("U%d" % i, 0, 16), 0.0)
+
+    def base_send(t, P):
+        ts(A("bs16", 0, 512), ind(A("brow", 0, P), A("snl%d" % t, 0, 32)), -1536, OP.add)
+        b = wb()
+        conv(b, [(0, 32, 1, "MD", rS("bs16", 0, 512))])
+        for s in range(2):
+            ts(A("xo", 16 * s, 16 * s + 16), A(b, 16 * s, 16 * s + 16), -1024 - 256 * s, OP.add)
+        ts(A("xz", 0, 32), A("xo", 0, 32), 0, OP.is_lt, 8192, OP.mult)
+        tt(A("xo2", 0, 32), A("xo", 0, 32), A("xz", 0, 32), OP.add)
+        ts(A("bo", 0, 32), A("xo2", 0, 32), 256, OP.min)
+        for s in order:
+            send(s, "b", A("bo", 16 * s, 16 * s + 16), "gbo", 16 * (1 - s), 16 * (1 - s) + 16)
+
+    def ghost0(t, P):
+        for i, s in enumerate(order):
+            o = A("sb0", 256 * s, 256 * s + 256)
+            x = ind(A("U0", OWN, OWN + P), A("snl%d" % t, 16 * s, 16 * s + 16))
+            if i == 0:
+                cp(o, x)
+            else:
+                act(o, x)
+        for s in order:
+            send(s, "0", A("sb0", 256 * s, 256 * s + 256), "U0", 16 + 256 * (1 - s), 16 + 256 * (1 - s) + 256)
+
+    def stlist(lo, t, leg, src):
+        nw, lw = NW[t], LW[t]
+        o = leg * lw + (32 if leg < 2 else 0)
+        for n in ("li%d" % t, "st%d" % t):
+            ts(A(n, o, o + nw), A(src, lo, lo + nw), 1536, OP.add)
+
+    base_send(0, V0)
+    b = wb()
+    conv(b, [(192, 288, 1, "MD", rS("ra", 0, V0)), (96, 192, 1, "MD", rS("rb", 0, V0)), (0, 96, 1, "MD", rS("rc", 0, V0))])
+    ghost0(0, V0)
+    cp(A("thf", 0, 1), A("thi", 0, 1))
+    cp(A("wtf", 0, 1), A("wti", 0, 1))
+    ts(A("pmod", 0, 160), A("pmi", 0, 160), 15, OP.bitwise_and)
+    tt(A("meS", 0, 160), A("pmod", 0, 160), A("c16", 0, 160), OP.add)
+    ts(A("slotc", 0, 32), A("meS", 0, 32), GH, OP.add)
+    for leg in (2, 1, 0):
+        stlist(96 * leg, 0, leg, b)
+    cb = (A("ab", 0, 1), A("ab", 1, 2))
+    ms(cb[0], -0.5)
+    ms(cb[1], 0.5)
+
+    def prep(t):
+        P, nw, lw = PP[t], NW[t], LW[t]
+        st, li = "st%d" % t, "li%d" % t
+        B0 = 2 * lw
+        ts(A("pl", 0, nw), A(st, B0, B0 + nw), P - 1, OP.min)
+        act(A("fr", 0, P), ind(A("brow", 0, P), A("pl", 0, nw)))
+        b = wb()
+        for i, nm in ((1, "rrow"), (0, "lrow")):
+            ts(A("ls16", 512 * i, 512 * i + 512), ind(A(nm, 0, P), A("snl%d" % t, 0, 32)), -1536, OP.add)
+            conv(b, [(32 * i, 32 * i + 32, 1, "MD", rS("ls16", 512 * i, 512 * i + 512))])
+        for s in range(2):
+            recv(s, "b", "gbo", 16 * s, 16 * s + 16)
+        for s in range(2):
+            act(A("brow", GH + 256 * s, GH + 256 * s + 256),
+                ind(A("snt", 272 * s, 272 * s + 272), A("gbo", 16 * s, 16 * s + 16)))
+        bl = b
+        b = wb()
+        h = lw // 2 + 16
+        for i, c0, c1 in ((1, 32, lw), (1, 0, 32), (0, 0, 32), (0, 32, h), (0, h, lw)):
+            nm = "gr%d" % i
+            tt(A(nm, 16 * c0, 16 * c1), ind(A("brow", 0, 3072), A(li, i * lw + c0, i * lw + c1)), A("mex", 16 * c0, 16 * c1), OP.is_equal)
+            if (i, c0) == (1, 32):
+                for n in (li, st):
+                    for k in range(2):
+                        ts(A(n, k * lw, k * lw + 32), A(bl, 32 * k, 32 * k + 32), 1536, OP.add)
+                ts(A("ixa", 0, 2 * lw), A(st, 0, 2 * lw), GH, OP.is_ge, -3072, OP.mult)
+                tt(A("ixb", 0, 2 * lw), A("ixa", 0, 2 * lw), A(st, 0, 2 * lw), OP.add)
+                ts(A("ixa", 0, 2 * lw), A("ixb", 0, 2 * lw), OWN, OP.add)
+            if (i, c0) == (0, h):
+                for k, d0, d1 in ((1, 0, lw), (0, 0, 32)):
+                    legs(b, k * lw + d0, k * lw + d1)
+                b1 = b
+                b = wb()
+            conv(b, [(i * lw + c0, i * lw + c1, 1, "MD", rS(nm, 16 * c0, 16 * c1))])
+        legs(b1, 32, h)
+        legs(b, h, lw)
+
+    def legs(b, lo, hi):
+        tt(A("ulf", lo, hi), A(b, lo, hi), A("ixa", lo, hi), OP.mult)
+        cp(A("ul", lo, hi), A("ulf", lo, hi))
+
+    held = {}
+
+    def turn(t):
+        P, nw = PP[t], NW[t]
+        b = wb()
+        conv(b, [(0, nw, 1, "MDf", rS("fr", 0, P))])
+        held["b"] = b
+
+    def pairs(t):
+        nw, lw = NW[t], LW[t]
+        st, B0 = "st%d" % t, 2 * LW[t]
+        b = held["b"]
+        ts(A("mB", 0, nw), A(st, B0, B0 + nw), GH, OP.is_lt, -88, OP.mult)
+        tt(A("mB2", 0, nw), A("meS", 0, nw), A(st, B0, B0 + nw), OP.is_lt)
+        tt(A("pe", 0, nw), A(b, 0, nw), A("meS", 0, nw), OP.is_equal)
+        tt(A("mB2", 0, nw), A("mB2", 0, nw), A("mB", 0, nw), OP.mult)
+        tt(A("mB", 0, nw), A("mB2", 0, nw), A("pe", 0, nw), OP.mult)
+        ts(A("thr", 0, nw), A("mB", 0, nw), 99, OP.add)
+
+    def flags_row(t, i):
+        P, nw, lw = PP[t], NW[t], LW[t]
+        o = i * lw + (32 if i < 2 else 0)
+        act(A("fr", 0, P), ind(A("rrow", 0, 3072), A("li%d" % t, o, o + nw)))
+        turn(t)
+
+    def flags_col(t, i):
+        nw, lw = NW[t], LW[t]
+        o = i * lw + (32 if i < 2 else 0)
+        b = held["b"]
+        tt(A("fl", nw * i, nw * i + nw), A(b, 0, nw), A("meS", 0, nw), OP.is_equal)
+        ts(A("pm2", nw * i, nw * i + nw), A("st%d" % t, o, o + nw), -GH, OP.add)
+
+    def flags_list(t):
+        nw, lw = NW[t], LW[t]
+        tt(A("lff", 0, 3 * nw), A("fl", 0, 3 * nw), A("pm2", 0, 3 * nw), OP.mult)
+        ts(A("lf", 0, 3 * nw), A("lff", 0, 3 * nw), GH, OP.add)
+        if t == 0:
+            tt(A("sna", 0, 32), A("st0", lw, lw + 32), A("slotc", 0, 32), OP.is_equal)
+            ts(A("snb", 0, 32), A("sn0", 0, 32), -GH, OP.add)
+            tt(A("snc", 0, 32), A("sna", 0, 32), A("snb", 0, 32), OP.mult)
+            ts(A("snf", 0, 32), A("snc", 0, 32), GH, OP.add)
+
+    def marks(u, lo, P, n):
+        nm = "in%d" % (n % 2)
+        for i in range(P // 512):
+            ts(A(nm, 512 * i, 512 * i + 512), A(u, lo + 512 * i, lo + 512 * i + 512), A("thf", 0, 1), OP.is_ge)
+            mm("p%d" % i, [(A("p%d" % i, 0, 512), A("eye", 0, 128), A(nm, 512 * i, 512 * i + 512), n == 0, n == 5)])
+
+    def depths(t, slack):
+        P, nw, lw = PP[t], NW[t], LW[t]
+        for n in range(5):
+            u = "U%d" % n
+            gr = "gr%d" % (n % 2)
+            win = A(u, 0, OWN + P)
+            marks(u, OWN, P, n)
+            for s in range(2):
+                recv(s, str(n), u, 16 + 256 * s, 16 + 256 * s + 256)
+            if n < 4:
+                for s in order:
+                    c = lw + 16 * s
+                    act(A(gr, 256 * s, 256 * s + 256), ind(win, A("ul", c, c + 16)))
+                for s in order:
+                    o = A("sb%d" % (n + 1), 256 * s, 256 * s + 256)
+                    tt(o, ind(win, A("ul", 16 * s, 16 * s + 16)), A(gr, 256 * s, 256 * s + 256), OP.max)
+                    send(s, str(n + 1), o, "U%d" % (n + 1), 16 + 256 * (1 - s), 16 + 256 * (1 - s) + 256)
+            H = P // 2
+            h16 = H // 16
+            for h in range(2):
+                c = lw + 32 + h16 * h
+                act(A(gr, 512 + H * h, 512 + H * h + H), ind(win, A("ul", c, c + h16)))
+            for h in range(2):
+                o = A("U%d" % (n + 1), OWN + H * h, OWN + H * h + H) if n < 4 else A("u5", H * h, H * h + H)
+                c = 32 + h16 * h
+                tt(o, ind(win, A("ul", c, c + h16)), A(gr, 512 + H * h, 512 + H * h + H), OP.max)
+            for f in slack.get(n, []):
+                f()
+        marks("u5", 0, P, 5)
+
+    def splits(t):
+        P, nw, nb = PP[t], NW[t], PP[t]
+        for i in range(P // 512):
+            o, x = A("in0", 512 * i, 512 * i + 512), A("p%d" % i, 0, 512)
+            if i % 2 == 0:
+                act(o, x, AF.Sign)
+            else:
+                ts(o, x, 0, OP.is_gt)
+        for i in range(P // 512):
+            act(A("in1", 512 * i, 512 * i + 512), A("p%d" % i, 0, 512), AF.Sign)
+        b = wb()
+        for c0, c1 in ((0, nw // 2), (nw // 2, nw)):
+            tt(A("gr1", 16 * c0, 16 * c1), ind(A("in0", 0, P), A("pl", c0, c1)), A("in1", 16 * c0, 16 * c1), OP.max)
+            conv(b, [(c0, c1, 1, "CQ", rS("gr1", 16 * c0, 16 * c1))])
+        tt(A("go", 0, nw), A(b, 0, nw), A("thr", 0, nw), OP.is_ge)
+        b = wb()
+        mm(b, [(A(b, nw, 2 * nw), A("blk", 0, 128), A("go", 0, nw), True, True),
+               (A(b, 0, nw), A("ltg", 0, 128), A("go", 0, nw), True, False),
+               (A(b, 0, nw), A("eye", 0, 128), A("me16", 0, nw), False, True)])
+        op("V", [lambda: g.vector.tensor_tensor_scan(X("sc", 0, nw), X(b, nw, 2 * nw), X("zer", 0, nw), 2048.0, OP.add, OP.add)],
+           [(b, 0, 512), ("zer", 0, nw)], [("sc", 0, nw)])
+        tt(A("ka", 0, nw), A("sc", 0, nw), A(b, 0, nw), OP.add)
+        tt(A("kc", 0, nw), A("ka", 0, nw), A("go", 0, nw), OP.mult)
+        tt(A("kd", 0, nw), A("kc", 0, nw), A("meS", 0, nw), OP.add)
+        cp(A("koff", 0, nw), A("kd", 0, nw))
+        scat(A("lrow", 0, 3072), A("koff", 0, nw), A("mex", 512, 512 + P))
+        ts((X("T16", 0, 512, 2), [("T16", 0, 512)]), A("lrow", 2048, 2304), -1536, OP.add)
+        b = wb()
+        conv(b, [(0, 16, 1, "MD", lambda q: (X("T16", 2 * q, 512, 32), [("T16", 0, 512)]))])
+        ts(A("tl", 0, 16), A(b, 0, 16), 1536, OP.add)
+        ts((X("T16", 1, 512, 2), [("T16", 0, 512)]), ind(A("brow", 0, nb + 512), A("tl", 0, 16)), -1536, OP.add)
+        b = wb()
+        conv(b, [(0, 32, 1, "MD", rS("T16", 0, 512))])
+        ts(A("TL", 0, 32), A(b, 0, 32), 1536, OP.add)
+        act(A("t32", 0, 32), A(b, 0, 32), AF.Identity, bias=1536.0)
+
+    def renames(t):
+        P, nw, nb = PP[t], NW[t], PP[t]
+        scat(A("NT", 0, nb + 512), A("TL", 0, 32), A("jrow", 0, 512))
+        act(A("eT", 0, 512), ind(A("U0", OWN, OWN + nb + 512), A("TL", 0, 32)))
+        win = A("NT", 0, 2576)
+        H = P // 2
+        act(A("vR", 0, P), ind(win, A("lf", nw, 2 * nw)))
+        act(A("vL", H, P), ind(win, A("lf", nw // 2, nw)))
+        act(A("vy", 0, 512), ind(A("vR", 0, nb + 512), A("TL", 0, 32)))
+        cp(A("vL", 0, H), ind(win, A("lf", 0, nw // 2)))
+        if t == 0:
+            cp(A("vs", 0, 512), ind(win, A("snf", 0, 32)))
+        cp(A("vB", 0, P), ind(win, A("lf", 2 * nw, 3 * nw)))
+        ts(A("Y16", 0, 512), ind(A("rrow", 0, nb + 512), A("TL", 0, 32)), -1536, OP.add)
+
+    def update(t, lay):
+        P, nw, nb = PP[t], NW[t], PP[t]
+        k0 = nb - 1.5
+        if lay == "S":
+            a, c, ic = "st%d" % t, "st%d" % (t + 1), LW[t + 1]
+            src = (32, LW[t] + 32, 2 * LW[t])
+            dst = (32, ic + 32, 2 * ic)
+        else:
+            a, c, ic = "ns%d" % t, "ns%d" % (t + 1), nw + 32
+            src = (0, nw, 2 * nw)
+            dst = (0, ic, 2 * ic)
+
+        def places(n, lo):
+            if lay == "S":
+                return [(lo, lo + nw, 1, "MD", rS(n, 0, P))]
+            r = [(lo, lo + 96, 1, "MD", lambda q: (X(n, 96 * q, 96 * q + 96), [(n, 0, P)]))]
+            if P > V0:
+                r.append((lo + 96, lo + 128, 1, "MD", lambda q: (X(n, V0 + 32 * q, V0 + 32 * q + 32), [(n, 0, P)])))
+            return r
+
+        def new(n, lo, swap):
+            if lay == "S":
+                return [(lo, lo + 32, 1, "MD", lambda q: (X(n, q ^ swap, 512, 16), [(n, 0, 512)]))]
+            if not swap:
+                return [(lo, lo + 32, 1, "MD", lambda q: (X(n, 32 * q, 32 * q + 32), [(n, 0, 512)]))]
+            return [(lo + e, lo + 32, 2, "MD", lambda q, e=e: (X(n, 32 * q + 1 - e, 32 * q + 32, 2), [(n, 0, 512)])) for e in range(2)]
+        for i in range(3):
+            act(A("pt", nw * i, nw * i + nw), A(a, src[i], src[i] + nw), AF.Identity, bias=-k0)
+        b = wb()
+        for n, lo in (("NT", 3 * nw), ("vR", nw), ("vL", 0), ("vB", 2 * nw)):
+            conv(b, places(n, lo))
+        b3 = wb()
+        act(A(b3, 0, 4 * nw), A(b, 0, 4 * nw), AF.Abs, bias=cb[0], scale=2.0)
+        ts(A("z", 0, 4 * nw), A(b, 0, 4 * nw), 0, OP.is_equal, -8192, OP.mult)
+        tt(A("q3", 0, 3 * nw), A(b3, 0, 3 * nw), A("z", 0, 3 * nw), OP.add)
+        ts(A("ysn", 0, nw), A(b3, 3 * nw, 4 * nw), k0, OP.add)
+        act(A(b3, 0, nw), A(b, 3 * nw, 4 * nw), AF.Abs, bias=cb[1], scale=2.0)
+        b2 = wb()
+        conv(b2, new("T16", 0, 0) + new("T16", 32, 1) + new("Y16", 64, 0) + new("vy", 96, 0))
+        tt(A("q3", 0, 3 * nw), A("q3", 0, 3 * nw), A("pt", 0, 3 * nw), OP.max)
+        ts(A("q3u", 0, 3 * nw), A("q3", 0, 3 * nw), k0, OP.add)
+        yield
+        ts(A("sp", 0, nw), A("z", 3 * nw, 4 * nw), 0, OP.is_equal)
+        ts(A("nsp", 0, nw), A("z", 3 * nw, 4 * nw), 0, OP.is_lt)
+        ts(A("ysn", nw, 2 * nw), A(b3, 0, nw), k0, OP.add)
+        for i in range(2):
+            tt(A("yss", nw * i, nw * i + nw), A("ysn", nw * i, nw * i + nw), A("sp", 0, nw), OP.mult)
+        tt(A("oc", 0, nw), A("q3u", 2 * nw, 3 * nw), A("nsp", 0, nw), OP.mult)
+        tt(A("od", 0, nw), A("q3u", 0, nw), A("sp", 0, nw), OP.mult)
+        tt(A(c, dst[2], dst[2] + nw), A("oc", 0, nw), A("od", 0, nw), OP.add)
+        o = nw
+        act(A(b3, 256, 288), A(b2, 96, 128), AF.Abs, bias=cb[0], scale=2.0)
+        act(A("yt", 0, 32), A(b2, 64, 96), AF.Identity, bias=1536 - k0)
+        act(A(c, dst[1] + o, dst[1] + o + 32), A(b2, 0, 32), AF.Identity, bias=1536.0)
+        act(A("tsw", 0, 32), A(b2, 32, 64), AF.Identity, bias=1536.0)
+        ts(A("zy", 0, 32), A(b2, 96, 128), 0, OP.is_equal, -8192, OP.mult)
+        tt(A("yzy", 0, 32), A(b3, 256, 288), A("zy", 0, 32), OP.add)
+        tt(A("td", 0, 32), A("yzy", 0, 32), A("yt", 0, 32), OP.max)
+        ts(A(c, dst[2] + o, dst[2] + o + 32), A("td", 0, 32), k0, OP.add)
+        yield
+        tt(A("oa", 0, nw), A("q3u", 0, nw), A("nsp", 0, nw), OP.mult)
+        tt(A(c, dst[0], dst[0] + nw), A("oa", 0, nw), A("yss", 0, nw), OP.add)
+        tt(A("ob", 0, nw), A("q3u", nw, 2 * nw), A("nsp", 0, nw), OP.mult)
+        tt(A(c, dst[1], dst[1] + nw), A("ob", 0, nw), A("yss", nw, 2 * nw), OP.add)
+        tr = A(c, dst[1] + o, dst[1] + o + 32)
+        ts(A("tab", 0, 32), tr, nb, OP.is_ge)
+        tt(A("td", 0, 32), tr, A("tsw", 0, 32), OP.subtract)
+        tt(A("yu", 0, 32), A("td", 0, 32), A("tab", 0, 32), OP.mult)
+        tt(A(c, dst[0] + o, dst[0] + o + 32), A("tsw", 0, 32), A("yu", 0, 32), OP.add)
+        yield
+
+    def srow(x, lo, ncol, row, both):
+        for i in range(ncol // 32):
+            b = wb()
+            mm(b, [(A(b, q, 512, 16), A("EQ", 128 * q, 128 * q + 128), A(x, lo + 32 * i, lo + 32 * i + 32), True, True) for q in range(16)])
+            o = A(row, 512 * i, 512 * i + 512)
+            if both and i % 2:
+                ts(o, A(b, 0, 512), 1536, OP.add)
+            else:
+                act(o, A(b, 0, 512), AF.Identity, bias=1536.0)
+
+    def new_snd():
+        b = wb()
+        conv(b, [(0, 32, 1, "MD", rS("vs", 0, 512))])
+        act(A("sna", 0, 32), A(b, 0, 32), AF.Abs, bias=cb[0], scale=2.0)
+        ts(A("snv", 0, 32), A(b, 0, 32), 0, OP.is_equal, -8192, OP.mult)
+        tt(A("snb", 0, 32), A("sna", 0, 32), A("snv", 0, 32), OP.add)
+        ts(A("snc", 0, 32), A("snb", 0, 32), V0 - 1.5, OP.add)
+        tt(A("sn1", 0, 32), A("snc", 0, 32), A("sn0", 0, 32), OP.max)
+        cp(A("snl1", 0, 32), A("sn1", 0, 32))
+        ts(A("sn16", 0, 32), A("sn1", 0, 32), -1536, OP.add)
+
+    def weigh(t):
+        nb = PP[t]
+        b = wb()
+        conv(b, [(0, 32, 1, "WQ", rS("eT", 0, 512))])
+        tt(A("hz", 0, 32), A(b, 0, 32), A("t32", 0, 32), OP.add)
+        tt(A("hz", 32, 64), A(b, 0, 32), A("meS", nb // 16, nb // 16 + 32), OP.add)
+
+    def children(t):
+        nb = PP[t]
+        ts(A("hz2", 0, 64), A("hz", 0, 64), 2047, OP.bitwise_and)
+        ts(A("hq", 0, 64), A("hz2", 0, 64), -2048, OP.add)
+        for i in range(2):
+            ts(A("pres", 32 * i, 32 * i + 32), A("t32", 0, 32), nb, OP.is_lt)
+        tt(A("hm", 0, 64), A("hq", 0, 64), A("pres", 0, 64), OP.mult)
+        ts(A("eo", 0, 64), A("hm", 0, 64), 2048, OP.add)
+        ts(A("e2", 0, 512), A("eT", 0, 512), 0.5, OP.mult, 128.75, OP.add)
+        ts(A("e2b", 0, 512), A("e2", 0, 512), -258, OP.add)
+        tt(A("cT", 0, 512), ind(A("dtb", 0, 2064), A("eo", 0, 32)), A("e2b", 0, 512), OP.add)
+        scat(A("U0", OWN, OWN + nb + 512), A("TL", 0, 32), A("cT", 0, 512))
+        tt(A("U0", OWN + nb, OWN + nb + 512), ind(A("dtb", 0, 2064), A("eo", 32, 64)), A("e2b", 0, 512), OP.add)
+
+    ms(A("rrow", GH, 3088), -1.0)
+    iota(A("rrow", V0, GH), [[1, 1024]], V0, 0)
+    iota(A("jq", 0, 256), [[1, 256]], 1, 0)
+    sel(A("tri", 0, 128), A("blk", 0, 128), [[-1, 128]], OP.is_ge, 0, 1)
+
+    def sentinels(t):
+        iota(A("lrow", 2048, 2304), [[2, 256]], PP[t], 0)
+
+    def late0():
+        for q in range(16):
+            act(A("MDf", 128 * q, 128 * q + 128), A("eye", 0, 128), AF.Copy, scale=A("pq", q, q + 1))
+        ts(A("ltg", 0, 128), A("tri", 0, 128), -1, OP.mult)
+        ts(A("me16", 0, 128), A("meS", 0, 128), -1, OP.mult)
+        ms(A("zer", 0, 128), 0.0)
+        cp((X("jrow", 0, 512, 2), [("jrow", 0, 512)]), A("jq", 0, 256))
+        ts((X("jrow", 1, 512, 2), [("jrow", 0, 512)]), A("jq", 0, 256), -1, OP.mult)
+
+    def masks2():
+        for i in range(4):
+            b = wb()
+            mm(b, [(A(b, 0, 512), A("blk", 0, 128), A("MD", 512 * i, 512 * i + 512), True, True)])
+            act(A("CQ", 512 * i, 512 * i + 512), A(b, 0, 512))
+            act(A("WQ", 512 * i, 512 * i + 512), A(b, 0, 512), AF.Copy, scale=A("wtf", 0, 1))
+
+    def late1():
+        ts(A("dtb", 0, 2048), A("dtb", 0, 2048), 0.5, OP.mult, 128.75, OP.add)
+        ms(A("dtb", 2048, 2064), 129.0)
+        ms(A("U0", OWN + V0, OWN + GH), 0.0)
+        cp(A("ns0", 0, 288), A("nraw", 0, 288))
+
+    def late2(t):
+        ms(A("NT", 0, 2576), 0.0)
+        ms(A("vR", PP[t], PP[t] + 512), 0.0)
+
+    prep(0)
+    depths(0, {0: [late0, lambda: turn(0), lambda: sentinels(0)], 1: [lambda: pairs(0), lambda: flags_row(0, 0), late1],
+               2: [lambda: flags_col(0, 0), lambda: flags_row(0, 1), lambda: late2(0)],
+               3: [lambda: flags_col(0, 1), lambda: flags_row(0, 2)], 4: [lambda: flags_col(0, 2), masks2, lambda: flags_list(0)]})
+    splits(0)
+    renames(0)
+    for _ in update(0, "S"):
+        pass
+    new_snd()
+    lw, nw = LW[1], NW[1]
+    ts(A("x16", 256, 384), A("st1", 2 * lw, 2 * lw + nw), -1536, OP.add)
+    srow("x16", 256, 128, "brow", True)
+    srow("sn16", 0, 32, "mex", False)
+    sndtab()
+    base_send(1, 2048)
+    for i in (1, 0):
+        ts(A("x16", 128 * i, 128 * i + 128), A("st1", lw * i + 32, lw * i + 32 + nw), -1536, OP.add)
+    weigh(0)
+    srow("x16", 128, 128, "rrow", False)
+    srow("x16", 0, 128, "lrow", False)
+    children(0)
+    ghost0(1, 2048)
+    for i in range(3):
+        o = lw * i + (32 if i < 2 else 0)
+        cp(A("li1", o, o + nw), A("st1", o, o + nw))
+    prep(1)
+    un = update(0, "N")
+    depths(1, {0: [lambda: turn(1), lambda: sentinels(1), lambda: next(un)],
+               1: [lambda: pairs(1), lambda: next(un), lambda: flags_row(1, 0)],
+               2: [lambda: flags_col(1, 0), lambda: next(un), lambda: flags_row(1, 1)],
+               3: [lambda: flags_col(1, 1), lambda: flags_row(1, 2), lambda: late2(1)], 4: [lambda: flags_col(1, 2), lambda: flags_list(1)]})
+    splits(1)
+    renames(1)
+    weigh(1)
+    children(1)
+    dma("Y", (HB("ye"), []), A("U0", OWN, OWN + GH))
+    for _ in update(1, "N"):
+        pass
+    for i, n in ((2, "yb"), (0, "yl"), (1, "yr")):
+        for j, (lo, hi, c0, c1) in enumerate(((0, 1536, 0, 96), (1536, 2048, 96, 128), (2048, 2560, 128, 160))):
+            dma("SYS"[j], (T[n][:, lo:hi], []), A("ns2", 160 * i + c0, 160 * i + c1))
+    wait_for("Y", {s: v for s, v in cnt.items()})

@@ -325,11 +325,11 @@ def rank_program(g, core, T, topo):
             ts(A(n, o, o + nw), A(src, lo, lo + nw), 1536, OP.add)
 
     base_send(0, V0)
+    cp(A("thf", 0, 1), A("thi", 0, 1))
+    cp(A("wtf", 0, 1), A("wti", 0, 1))
     b = wb()
     conv(b, [(192, 288, 1, "MD", rS("ra", 0, V0)), (96, 192, 1, "MD", rS("rb", 0, V0)), (0, 96, 1, "MD", rS("rc", 0, V0))])
     ghost0(0, V0)
-    cp(A("thf", 0, 1), A("thi", 0, 1))
-    cp(A("wtf", 0, 1), A("wti", 0, 1))
     ts(A("pmod", 0, 160), A("pmi", 0, 160), 15, OP.bitwise_and)
     tt(A("meS", 0, 160), A("pmod", 0, 160), A("c16", 0, 160), OP.add)
     ts(A("slotc", 0, 32), A("meS", 0, 32), GH, OP.add)
@@ -345,36 +345,39 @@ def rank_program(g, core, T, topo):
         B0 = 2 * lw
         ts(A("pl", 0, nw), A(st, B0, B0 + nw), P - 1, OP.min)
         act(A("fr", 0, P), ind(A("brow", 0, P), A("pl", 0, nw)))
-        b = wb()
+        if t == 0:
+            masks2()
+        h = lw // 2 + 16
+
+        def valid(b, i, c0, c1):
+            nm = "gr%d" % i
+            tt(A(nm, 16 * c0, 16 * c1), ind(A("brow", 0, 3072), A(li, i * lw + c0, i * lw + c1)), A("mex", 16 * c0, 16 * c1), OP.is_equal)
+            conv(b, [(i * lw + c0, i * lw + c1, 1, "MD", rS(nm, 16 * c0, 16 * c1))])
+        b, bl, b1 = wb(), wb(), wb()
+        valid(b, 1, 32, lw)
         for i, nm in ((1, "rrow"), (0, "lrow")):
             ts(A("ls16", 512 * i, 512 * i + 512), ind(A(nm, 0, P), A("snl%d" % t, 0, 32)), -1536, OP.add)
-            conv(b, [(32 * i, 32 * i + 32, 1, "MD", rS("ls16", 512 * i, 512 * i + 512))])
+            conv(bl, [(32 * i, 32 * i + 32, 1, "MD", rS("ls16", 512 * i, 512 * i + 512))])
+        valid(b, 0, 32, h)
+        for k in (1, 0):
+            ts(A(li, k * lw, k * lw + 32), A(bl, 32 * k, 32 * k + 32), 1536, OP.add)
+            ts(A(st, k * lw, k * lw + 32), A(bl, 32 * k, 32 * k + 32), 1536, OP.add)
+        ts(A("ixa", 0, 2 * lw), A(st, 0, 2 * lw), GH, OP.is_ge, -3072, OP.mult)
+        tt(A("ixb", 0, 2 * lw), A("ixa", 0, 2 * lw), A(st, 0, 2 * lw), OP.add)
+        ts(A("ixa", 0, 2 * lw), A("ixb", 0, 2 * lw), OWN, OP.add)
+        valid(b, 1, 0, 32)
+        valid(b, 0, 0, 32)
+        valid(b1, 0, h, lw)
+        legs(b, lw, 2 * lw)
+        legs(b, 0, h)
+        legs(b1, h, lw)
+
+    def ghost_bases():
         for s in range(2):
             recv(s, "b", "gbo", 16 * s, 16 * s + 16)
         for s in range(2):
             act(A("brow", GH + 256 * s, GH + 256 * s + 256),
                 ind(A("snt", 272 * s, 272 * s + 272), A("gbo", 16 * s, 16 * s + 16)))
-        bl = b
-        b = wb()
-        h = lw // 2 + 16
-        for i, c0, c1 in ((1, 32, lw), (1, 0, 32), (0, 0, 32), (0, 32, h), (0, h, lw)):
-            nm = "gr%d" % i
-            tt(A(nm, 16 * c0, 16 * c1), ind(A("brow", 0, 3072), A(li, i * lw + c0, i * lw + c1)), A("mex", 16 * c0, 16 * c1), OP.is_equal)
-            if (i, c0) == (1, 32):
-                for n in (li, st):
-                    for k in range(2):
-                        ts(A(n, k * lw, k * lw + 32), A(bl, 32 * k, 32 * k + 32), 1536, OP.add)
-                ts(A("ixa", 0, 2 * lw), A(st, 0, 2 * lw), GH, OP.is_ge, -3072, OP.mult)
-                tt(A("ixb", 0, 2 * lw), A("ixa", 0, 2 * lw), A(st, 0, 2 * lw), OP.add)
-                ts(A("ixa", 0, 2 * lw), A("ixb", 0, 2 * lw), OWN, OP.add)
-            if (i, c0) == (0, h):
-                for k, d0, d1 in ((1, 0, lw), (0, 0, 32)):
-                    legs(b, k * lw + d0, k * lw + d1)
-                b1 = b
-                b = wb()
-            conv(b, [(i * lw + c0, i * lw + c1, 1, "MD", rS(nm, 16 * c0, 16 * c1))])
-        legs(b1, 32, h)
-        legs(b, h, lw)
 
     def legs(b, lo, hi):
         tt(A("ulf", lo, hi), A(b, lo, hi), A("ixa", lo, hi), OP.mult)
@@ -460,14 +463,13 @@ def rank_program(g, core, T, topo):
 
     def splits(t):
         P, nw, nb = PP[t], NW[t], PP[t]
-        for i in range(P // 512):
-            o, x = A("in0", 512 * i, 512 * i + 512), A("p%d" % i, 0, 512)
-            if i % 2 == 0:
-                act(o, x, AF.Sign)
-            else:
-                ts(o, x, 0, OP.is_gt)
-        for i in range(P // 512):
-            act(A("in1", 512 * i, 512 * i + 512), A("p%d" % i, 0, 512), AF.Sign)
+        for k in range(2):
+            for i in range(P // 512):
+                o, x = A("in%d" % k, 512 * i, 512 * i + 512), A("p%d" % i, 0, 512)
+                if (i + k) % 2 == 0:
+                    act(o, x, AF.Sign)
+                else:
+                    ts(o, x, 0, OP.is_gt)
         b = wb()
         for c0, c1 in ((0, nw // 2), (nw // 2, nw)):
             tt(A("gr1", 16 * c0, 16 * c1), ind(A("in0", 0, P), A("pl", c0, c1)), A("in1", 16 * c0, 16 * c1), OP.max)
@@ -502,11 +504,13 @@ def rank_program(g, core, T, topo):
         H = P // 2
         act(A("vR", 0, P), ind(win, A("lf", nw, 2 * nw)))
         act(A("vL", H, P), ind(win, A("lf", nw // 2, nw)))
+        act(A("e2", 0, 512), A("eT", 0, 512), AF.Identity, bias=128.75, scale=0.5)
+        act(A("e2b", 0, 512), A("e2", 0, 512), AF.Identity, bias=-258.0)
         act(A("vy", 0, 512), ind(A("vR", 0, nb + 512), A("TL", 0, 32)))
+        cp(A("vB", 0, P), ind(win, A("lf", 2 * nw, 3 * nw)))
         cp(A("vL", 0, H), ind(win, A("lf", 0, nw // 2)))
         if t == 0:
             cp(A("vs", 0, 512), ind(win, A("snf", 0, 32)))
-        cp(A("vB", 0, P), ind(win, A("lf", 2 * nw, 3 * nw)))
         ts(A("Y16", 0, 512), ind(A("rrow", 0, nb + 512), A("TL", 0, 32)), -1536, OP.add)
 
     def update(t, lay):
@@ -538,16 +542,16 @@ def rank_program(g, core, T, topo):
         for i in range(3):
             act(A("pt", nw * i, nw * i + nw), A(a, src[i], src[i] + nw), AF.Identity, bias=-k0)
         b = wb()
-        for n, lo in (("NT", 3 * nw), ("vR", nw), ("vL", 0), ("vB", 2 * nw)):
+        for n, lo in (("NT", 3 * nw), ("vB", 2 * nw), ("vR", nw), ("vL", 0)):
             conv(b, places(n, lo))
-        b3 = wb()
+        b3, b2 = wb(), wb()
+        conv(b2, new("T16", 0, 0) + new("T16", 32, 1) + new("Y16", 64, 0) + new("vy", 96, 0))
+        yield
         act(A(b3, 0, 4 * nw), A(b, 0, 4 * nw), AF.Abs, bias=cb[0], scale=2.0)
         ts(A("z", 0, 4 * nw), A(b, 0, 4 * nw), 0, OP.is_equal, -8192, OP.mult)
         tt(A("q3", 0, 3 * nw), A(b3, 0, 3 * nw), A("z", 0, 3 * nw), OP.add)
         ts(A("ysn", 0, nw), A(b3, 3 * nw, 4 * nw), k0, OP.add)
         act(A(b3, 0, nw), A(b, 3 * nw, 4 * nw), AF.Abs, bias=cb[1], scale=2.0)
-        b2 = wb()
-        conv(b2, new("T16", 0, 0) + new("T16", 32, 1) + new("Y16", 64, 0) + new("vy", 96, 0))
         tt(A("q3", 0, 3 * nw), A("q3", 0, 3 * nw), A("pt", 0, 3 * nw), OP.max)
         ts(A("q3u", 0, 3 * nw), A("q3", 0, 3 * nw), k0, OP.add)
         yield
@@ -616,8 +620,6 @@ def rank_program(g, core, T, topo):
             ts(A("pres", 32 * i, 32 * i + 32), A("t32", 0, 32), nb, OP.is_lt)
         tt(A("hm", 0, 64), A("hq", 0, 64), A("pres", 0, 64), OP.mult)
         ts(A("eo", 0, 64), A("hm", 0, 64), 2048, OP.add)
-        ts(A("e2", 0, 512), A("eT", 0, 512), 0.5, OP.mult, 128.75, OP.add)
-        ts(A("e2b", 0, 512), A("e2", 0, 512), -258, OP.add)
         tt(A("cT", 0, 512), ind(A("dtb", 0, 2064), A("eo", 0, 32)), A("e2b", 0, 512), OP.add)
         scat(A("U0", OWN, OWN + nb + 512), A("TL", 0, 32), A("cT", 0, 512))
         tt(A("U0", OWN + nb, OWN + nb + 512), ind(A("dtb", 0, 2064), A("eo", 32, 64)), A("e2b", 0, 512), OP.add)
@@ -626,6 +628,7 @@ def rank_program(g, core, T, topo):
     iota(A("rrow", V0, GH), [[1, 1024]], V0, 0)
     iota(A("jq", 0, 256), [[1, 256]], 1, 0)
     sel(A("tri", 0, 128), A("blk", 0, 128), [[-1, 128]], OP.is_ge, 0, 1)
+    iota(A("U0", OWN + V0, OWN + GH), [[0, 1024]], 0, 0)
 
     def sentinels(t):
         iota(A("lrow", 2048, 2304), [[2, 256]], PP[t], 0)
@@ -647,19 +650,20 @@ def rank_program(g, core, T, topo):
             act(A("WQ", 512 * i, 512 * i + 512), A(b, 0, 512), AF.Copy, scale=A("wtf", 0, 1))
 
     def late1():
-        ts(A("dtb", 0, 2048), A("dtb", 0, 2048), 0.5, OP.mult, 128.75, OP.add)
+        act(A("dtb", 0, 2048), A("dtb", 0, 2048), AF.Identity, bias=128.75, scale=0.5)
         ms(A("dtb", 2048, 2064), 129.0)
-        ms(A("U0", OWN + V0, OWN + GH), 0.0)
         cp(A("ns0", 0, 288), A("nraw", 0, 288))
 
     def late2(t):
-        ms(A("NT", 0, 2576), 0.0)
-        ms(A("vR", PP[t], PP[t] + 512), 0.0)
+        iota(A("NT", 0, 2576), [[0, 2576]], 0, 0)
+        iota(A("vR", PP[t], PP[t] + 512), [[0, 512]], 0, 0)
 
+    ghost_bases()
     prep(0)
-    depths(0, {0: [late0, lambda: turn(0), lambda: sentinels(0)], 1: [lambda: pairs(0), lambda: flags_row(0, 0), late1],
-               2: [lambda: flags_col(0, 0), lambda: flags_row(0, 1), lambda: late2(0)],
-               3: [lambda: flags_col(0, 1), lambda: flags_row(0, 2)], 4: [lambda: flags_col(0, 2), masks2, lambda: flags_list(0)]})
+    depths(0, {0: [late0, lambda: turn(0), lambda: sentinels(0)], 1: [lambda: pairs(0), lambda: flags_row(0, 0)],
+               2: [lambda: flags_col(0, 0), lambda: flags_row(0, 1)],
+               3: [lambda: flags_col(0, 1), lambda: flags_row(0, 2), lambda: late2(0)],
+               4: [late1, lambda: flags_col(0, 2), lambda: flags_list(0)]})
     splits(0)
     renames(0)
     for _ in update(0, "S"):
@@ -675,6 +679,7 @@ def rank_program(g, core, T, topo):
         ts(A("x16", 128 * i, 128 * i + 128), A("st1", lw * i + 32, lw * i + 32 + nw), -1536, OP.add)
     weigh(0)
     srow("x16", 128, 128, "rrow", False)
+    ghost_bases()
     srow("x16", 0, 128, "lrow", False)
     children(0)
     ghost0(1, 2048)
@@ -683,10 +688,11 @@ def rank_program(g, core, T, topo):
         cp(A("li1", o, o + nw), A("st1", o, o + nw))
     prep(1)
     un = update(0, "N")
-    depths(1, {0: [lambda: turn(1), lambda: sentinels(1), lambda: next(un)],
-               1: [lambda: pairs(1), lambda: next(un), lambda: flags_row(1, 0)],
+    next(un)
+    depths(1, {0: [lambda: turn(1), lambda: sentinels(1), lambda: next(un)], 1: [lambda: pairs(1), lambda: flags_row(1, 0)],
                2: [lambda: flags_col(1, 0), lambda: next(un), lambda: flags_row(1, 1)],
-               3: [lambda: flags_col(1, 1), lambda: flags_row(1, 2), lambda: late2(1)], 4: [lambda: flags_col(1, 2), lambda: flags_list(1)]})
+               3: [lambda: flags_col(1, 1), lambda: next(un), lambda: flags_row(1, 2), lambda: late2(1)],
+               4: [lambda: flags_col(1, 2), lambda: flags_list(1)]})
     splits(1)
     renames(1)
     weigh(1)

import numpy as np
from concourse.mybir import dt, AluOpType, AxisListType, ActivationFunctionType

OP = AluOpType
AF = ActivationFunctionType
NR = 4
V0 = 1536
GH = 2560
OWN = 528

SCRATCH = {}
PK = {}


def _pack(big, dtype, parts):
    o = 0
    for n, c in parts:
        PK[n] = (big, o)
        o += (c + 15) // 16 * 16
    SCRATCH[big] = ("sbuf", [128, o], dtype)


_pack("kf", "float32", (("pq", 16), ("meS", 160), ("slotc", 32), ("zer", 128), ("thf", 1), ("wtf", 1), ("ab", 2),
                        ("st0", 352), ("st1", 448), ("ns0", 288), ("ns1", 384), ("ns2", 480), ("sn0", 32), ("sn1", 32),
                        ("ixa", 320), ("ixb", 320), ("ulf", 320), ("mB", 128), ("mB2", 128), ("pe", 128), ("thr", 128),
                        ("xo", 32), ("xz", 32), ("xo2", 32), ("sc", 128), ("ka", 128), ("kc", 128), ("kd", 128),
                        ("pm2", 384), ("fl", 384), ("lff", 384), ("t32", 32), ("z", 512), ("pt", 384), ("q3", 384),
                        ("q3u", 384), ("sp", 128), ("nsp", 128), ("ysn", 256), ("yss", 256), ("oa", 128), ("ob", 128),
                        ("oc", 128), ("od", 128), ("tsw", 32), ("tab", 32), ("td", 32), ("zy", 32), ("yzy", 32), ("yt", 32),
                        ("yu", 32), ("snv", 32), ("sna", 32), ("snb", 32), ("snc", 32), ("hq", 64), ("hm", 64), ("pres", 64)))
_pack("ki", "int32", (("nraw", 288), ("nsn", 32), ("thi", 1), ("wti", 1), ("ik", 16), ("ik2", 16), ("pmi", 160), ("pmod", 160),
                      ("c16", 160), ("hz", 64), ("hz2", 64)))
_pack("ku", "uint16", (("li0", 352), ("li1", 448), ("snl0", 32), ("snl1", 32), ("gbo", 32), ("bo", 32), ("ul", 320), ("pl", 128),
                       ("koff", 128), ("tl", 16), ("TL", 32), ("lf", 384), ("snf", 32), ("eo", 64)))
_pack("kh", "float16", (("n16", 288), ("nsn16", 32), ("ra", 1536), ("rb", 1536), ("rc", 1536), ("bs16", 512), ("ls16", 1024),
                        ("T16", 512), ("Y16", 512), ("x16", 384), ("sn16", 32), ("me16", 128)))
_pack("kb", "bfloat16", (("ones", 128), ("eye", 128), ("blk", 128), ("blka", 128), ("tri", 128), ("ltg", 128), ("jq", 256),
                         ("jrow", 512), ("go", 128), ("eT", 512), ("e2", 512), ("e2b", 512), ("cT", 512), ("vs", 512), ("vy", 512),
                         ("sb0", 512), ("sb1", 512), ("sb2", 512), ("sb3", 512), ("sb4", 512)))
for _n, _c, _d in (("brow", 3088, "float32"), ("lrow", 3088, "float32"), ("rrow", 3088, "float32"), ("mex", 2560, "float32"),
                   ("snt", 544, "float32"), ("fr", 2048, "float32"), ("MDf", 2048, "float32"),
                   ("MD", 2048, "bfloat16"), ("EQ", 2048, "bfloat16"), ("CQ", 2048, "bfloat16"), ("WQ", 2048, "bfloat16"),
                   ("dtb", 2064, "bfloat16"), ("NT", 2576, "bfloat16"), ("vL", 2048, "bfloat16"), ("vR", 2560, "bfloat16"),
                   ("vB", 2048, "bfloat16"), ("U0", OWN + 2560, "bfloat16"), ("U1", OWN + 2048, "bfloat16"),
                   ("U2", OWN + 2048, "bfloat16"), ("U3", OWN + 2048, "bfloat16"), ("U4", OWN + 2048, "bfloat16"),
                   ("u5", 2048, "bfloat16"), ("gr0", 2560, "bfloat16"), ("gr1", 2560, "bfloat16"), ("in0", 2048, "bfloat16"),
                   ("in1", 2048, "bfloat16")):
    SCRATCH[_n] = ("sbuf", [128, _c], _d)
for _n in range(8):
    SCRATCH["p%d" % _n] = ("psum", [128, 512], "float32")

KINDS = ["b", "0", "1", "2", "3", "4"]
SEMAPHORES = (["cv", "cs", "cp", "cg"] + ["d%d" % i for i in range(24)]
              + ["r%s%d" % (k, s) for k in KINDS for s in range(2)] + ["l%s%d" % (k, s) for k in KINDS for s in range(2)])


def _is_psum(n):
    return len(n) == 2 and n[0] == "p" and n[1].isdigit()


def rank_program(g, core, T, topo):
    rank = T.rank_of(core)
    if rank is None:
        return
    nb_core = [T.cores[(rank - 1) % NR], T.cores[(rank + 1) % NR]]
    order = sorted(range(2), key=lambda s: nb_core[s] in topo.cores_of(core))

    Q = {"V": g.vector, "S": g.scalar, "P": g.tensor, "G": g, "Y": g.sync}
    SEM = {"V": "cv", "S": "cs", "P": "cp", "G": "cg"}
    cnt = {}
    known = {q: {} for q in Q}
    snaps = {}
    hist = {}

    def wait_for(q, need):
        for s in sorted(need):
            v = need[s]
            if known[q].get(s, 0) >= v:
                continue
            Q[q].wait_ge(T.sem[s], v)
            known[q][s] = v
            for s2, v2 in snaps.get((s, v), {}).items():
                if known[q].get(s2, 0) < v2:
                    known[q][s2] = v2

    def needs(q, reads, writes):
        need = {}
        for regs, w in ((reads, 0), (writes, 1)):
            for n, lo, hi in regs:
                ps = _is_psum(n)
                for e in hist.get(n, []):
                    if not ps and (e[0] >= hi or lo >= e[1]):
                        continue
                    if ps:
                        if e[5] == q and (q == "P" or not (w or e[2])):
                            continue
                    elif not (w or e[2]):
                        continue
                    if need.get(e[3], 0) < e[4]:
                        need[e[3]] = e[4]
        return need

    def note(q, reads, writes, sem, val):
        snaps[(sem, val)] = dict(known[q]) if q else {}
        for regs, w in ((writes, 1), (reads, 0)):
            for n, lo, hi in regs:
                old = hist.get(n, [])
                if w:
                    old = [e for e in old if not (lo <= e[0] and e[1] <= hi)]
                else:
                    old = [e for e in old if not (e[2] == 0 and e[3] == sem and lo <= e[0] and e[1] <= hi)]
                old.append((lo, hi, w, sem, val, q))
                hist[n] = old

    def op(q, fns, reads, writes):
        wait_for(q, needs(q, reads, writes))
        s = SEM[q]
        for f in fns:
            f().then_inc(T.sem[s], 1)
            cnt[s] = cnt.get(s, 0) + 1
        note(q, reads, writes, s, cnt[s])

    ndma = [0]

    def dma(q, out, in_):
        wait_for(q, needs(q, in_[1], out[1]))
        s = "d%d" % ndma[0]
        ndma[0] += 1
        Q[q].dma_start(out[0], in_[0]).then_inc(T.sem[s], 16)
        cnt[s] = 16
        note(q, in_[1], out[1], s, 16)

    def X(n, lo, hi, st=1):
        if n in PK:
            t, o = T[PK[n][0]], PK[n][1]
        else:
            t, o = T[n], 0
        return t[:, o + lo:o + hi] if st == 1 else t[:, o + lo:o + hi:st]

    def A(n, lo, hi, st=1):
        return (X(n, lo, hi, st), [(n, lo, hi)])

    def ind(w, o):
        return (w[0].indirect(o[0]), w[1] + o[1])

    def tt(out, a, b, f):
        op("V", [lambda: g.vector.tensor_tensor(out[0], a[0], b[0], f)], a[1] + b[1], out[1])

    def ts(out, a, s1, f1, s2=None, f2=None):
        r = list(a[1])
        v1 = s1
        if isinstance(s1, tuple):
            r += s1[1]
            v1 = s1[0]
        if f2 is None:
            op("V", [lambda: g.vector.tensor_scalar(out[0], a[0], v1, None, f1)], r, out[1])
        else:
            op("V", [lambda: g.vector.tensor_scalar(out[0], a[0], v1, s2, f1, f2)], r, out[1])

    def cp(out, a):
        op("V", [lambda: g.vector.tensor_copy(out[0], a[0])], a[1], out[1])

    def scat(w, o, a):
        op("V", [lambda: g.vector.tensor_copy(w[0].indirect(o[0]), a[0])], a[1] + o[1], w[1])

    def ms(out, v):
        op("V", [lambda: g.vector.memset(out[0], v)], [], out[1])

    def act(out, a, f=AF.Copy, bias=0.0, scale=1.0):
        r = list(a[1])
        sc = scale
        if isinstance(scale, tuple):
            r += scale[1]
            sc = scale[0]
        bi = bias
        if isinstance(bias, tuple):
            r += bias[1]
            bi = bias[0]
        op("S", [lambda: g.scalar.activation(out[0], a[0], f, bias=bi, scale=sc)], r, out[1])

    def iota(out, pattern, base, cm, small=True):
        if small:
            op("G", [lambda: g.iota(out[0], pattern, base, cm, allow_small_or_imprecise_dtypes=True)], [], out[1])
        else:
            op("G", [lambda: g.iota(out[0], pattern, base, cm)], [], out[1])

    def sel(out, a, pattern, cmp, base, cm):
        op("G", [lambda: g.affine_select(out[0], a[0], pattern, cmp, 0.0, base, cm)], a[1], out[1])

    bank = [4]

    def wb():
        b = bank[0]
        bank[0] = 4 + (b - 3) % 4
        return "p%d" % b

    def mm(b, jobs):
        fns, rd = [], []
        for o, l, r, s0, s1 in jobs:
            fns.append(lambda o=o, l=l, r=r, s0=s0, s1=s1: g.tensor.matmul(o[0], l[0], r[0], s0, s1))
            for x in (l, r):
                if x[1][0] not in rd:
                    rd.append(x[1][0])
        op("P", fns, rd, [(b, 0, 512)])

    def conv(b, jobs):
        js = []
        for lo, hi, st, m, rh in jobs:
            for q in range(16):
                js.append((A(b, lo, hi, st), A(m, 128 * q, 128 * q + 128), rh(q), q == 0, q == 15))
        mm(b, js)

    def rS(n, lo, hi):
        return lambda q: (X(n, lo + q, hi, 16), [(n, lo, hi)])

    def chosen(src, dst):
        return topo.engines(src, dst)[-8:]

    def send(s, kind, src, dst, lo, hi):
        d = nb_core[s]
        wait_for("G", needs("G", src[1], []))
        rid, pid = topo.addr(d, core)
        es = chosen(core, d)
        ls = "l%s%d" % (kind, s)
        g.remote_dma(X(dst, lo, hi), src[0], T.sem["r%s%d" % (kind, 1 - s)], T.sem[ls], pid, rid, sum(1 << e for e in es))
        cnt[ls] = cnt.get(ls, 0) + len(es)
        note("G", src[1], [], ls, cnt[ls])

    def recv(s, kind, dst, lo, hi):
        rs = "r%s%d" % (kind, s)
        cnt[rs] = cnt.get(rs, 0) + len(chosen(nb_core[s], core))
        note(None, [], [(dst, lo, hi)], rs, cnt[rs])

    def HB(n):
        return T[n][:]

    PP, NW, LW = (V0, 2048), (96, 128), (128, 160)

    dma("Y", A("nsn", 0, 32), (HB("snd"), []))
    dma("S", A("nraw", 192, 288), (HB("bs"), []))
    dma("Y", A("nraw", 96, 192), (HB("rt"), []))
    dma("S", A("nraw", 0, 96), (HB("lt"), []))
    dma("Y", A("U0", OWN, OWN + V0), (HB("err"), []))
    dma("S", A("thi", 0, 1), (HB("th"), []))
    dma("S", A("wti", 0, 1), (HB("wt"), []))
    dma("Y", A("dtb", 0, 2048), (HB("det"), []))

    ms(A("ones", 0, 128), 1.0)
    iota(A("ik", 0, 16), [[-1, 16]], 16, 1, False)
    sel(A("blka", 0, 128), A("ones", 0, 128), [[-16, 8], [0, 16]], OP.is_ge, 0, 1)
    sel(A("blk", 0, 128), A("blka", 0, 128), [[16, 8], [0, 16]], OP.is_ge, 15, -1)
    sel(A("eye", 0, 128), A("ones", 0, 128), [[-1, 128]], OP.is_equal, 0, 1)
    iota(A("pmi", 0, 160), [[0, 160]], 0, 1, False)
    iota(A("c16", 0, 160), [[16, 160]], 0, 0, False)
    iota(A("brow", V0, GH), [[2, 512], [-1, 2]], V0 + 1, 0)
    iota(A("mex", 512, 2560), [[1, 2048]], 0, 0)
    ts(A("ik2", 0, 16), A("ik", 0, 16), 15, OP.bitwise_and)
    ts(A("pq", 0, 16), A("ik2", 0, 16), 0, OP.is_equal)
    for q in range(16):
        ts(A("EQ", 128 * q, 128 * q + 128), A("blk", 0, 128), A("pq", q, q + 1), OP.mult)
        act(A("MD", 128 * q, 128 * q + 128), A("eye", 0, 128), AF.Copy, scale=A("pq", q, q + 1))
    ts(A("nsn16", 0, 32), A("nsn", 0, 32), -1536, OP.add)
    ts(A("n16", 192, 288), A("nraw", 192, 288), -1536, OP.add)
    ts(A("n16", 0, 192), A("nraw", 0, 192), -1536, OP.add)

    def nrow(x, lo, row, r16):
        for i in range(4):
            b = wb()
            k = min(5, 16 - 5 * i)
            mm(b, [(A(b, 96 * j, 96 * j + 96), A("EQ", 128 * (5 * i + j), 128 * (5 * i + j) + 128), A(x, lo, lo + 96), True, True)
                   for j in range(k)])
            act(A(row, 480 * i, 480 * i + 96 * k), A(b, 0, 96 * k), AF.Identity, bias=1536.0)
            cp(A(r16, 480 * i, 480 * i + 96 * k), A(b, 0, 96 * k))

    b = wb()
    mm(b, [(A(b, 32 * q, 32 * q + 32), A("EQ", 128 * q, 128 * q + 128), A("nsn16", 0, 32), True, True) for q in range(16)])
    cp(A("bs16", 0, 512), A(b, 0, 512))
    sb = b
    b = wb()
    conv(b, [(0, 32, 1, "MD", rS("bs16", 0, 512))])
    ts(A("snl0", 0, 32), A(b, 0, 32), 1536, OP.add)
    ts(A("sn0", 0, 32), A(b, 0, 32), 1536, OP.add)
    act(A("mex", 0, 512), A(sb, 0, 512), AF.Identity, bias=1536.0)

    def sndtab():
        for s in range(2):
            act(A("snt", 272 * s, 272 * s + 256), A("mex", 256 * s, 256 * s + 256))

    nrow("n16", 192, "brow", "ra")
    nrow("n16", 96, "rrow", "rb")
    nrow("n16", 0, "lrow", "rc")
    sndtab()
    ms(A("snt", 256, 272), -1.0)
    ms(A("snt", 528, 544), -1.0)
    for i in range(5):
        ms(A("U%d" % i, 0, 16), 0.0)

    def base_send(t, P):
        ts(A("bs16", 0, 512), ind(A("brow", 0, P), A("snl%d" % t, 0, 32)), -1536, OP.add)
        b = wb()
        conv(b, [(0, 32, 1, "MD", rS("bs16", 0, 512))])
        for s in range(2):
            ts(A("xo", 16 * s, 16 * s + 16), A(b, 16 * s, 16 * s + 16), -1024 - 256 * s, OP.add)
        ts(A("xz", 0, 32), A("xo", 0, 32), 0, OP.is_lt, 8192, OP.mult)
        tt(A("xo2", 0, 32), A("xo", 0, 32), A("xz", 0, 32), OP.add)
        ts(A("bo", 0, 32), A("xo2", 0, 32), 256, OP.min)
        for s in order:
            send(s, "b", A("bo", 16 * s, 16 * s + 16), "gbo", 16 * (1 - s), 16 * (1 - s) + 16)

    def ghost0(t, P):
        for i, s in enumerate(order):
            o = A("sb0", 256 * s, 256 * s + 256)
            x = ind(A("U0", OWN, OWN + P), A("snl%d" % t, 16 * s, 16 * s + 16))
            if i == 0:
                cp(o, x)
            else:
                act(o, x)
        for s in order:
            send(s, "0", A("sb0", 256 * s, 256 * s + 256), "U0", 16 + 256 * (1 - s), 16 + 256 * (1 - s) + 256)

    def stlist(lo, t, leg, src):
        nw, lw = NW[t], LW[t]
        o = leg * lw + (32 if leg < 2 else 0)
        for n in ("li%d" % t, "st%d" % t):
            ts(A(n, o, o + nw), A(src, lo, lo + nw), 1536, OP.add)

    base_send(0, V0)
    cp(A("thf", 0, 1), A("thi", 0, 1))
    cp(A("wtf", 0, 1), A("wti", 0, 1))
    b = wb()
    conv(b, [(192, 288, 1, "MD", rS("ra", 0, V0)), (96, 192, 1, "MD", rS("rb", 0, V0)), (0, 96, 1, "MD", rS("rc", 0, V0))])
    ghost0(0, V0)
    ts(A("pmod", 0, 160), A("pmi", 0, 160), 15, OP.bitwise_and)
    tt(A("meS", 0, 160), A("pmod", 0, 160), A("c16", 0, 160), OP.add)
    ts(A("slotc", 0, 32), A("meS", 0, 32), GH, OP.add)
    for leg in (2, 1, 0):
        stlist(96 * leg, 0, leg, b)
    cb = (A("ab", 0, 1), A("ab", 1, 2))
    ms(cb[0], -0.5)
    ms(cb[1], 0.5)

    def prep(t):
        P, nw, lw = PP[t], NW[t], LW[t]
        st, li = "st%d" % t, "li%d" % t
        B0 = 2 * lw
        ts(A("pl", 0, nw), A(st, B0, B0 + nw), P - 1, OP.min)
        act(A("fr", 0, P), ind(A("brow", 0, P), A("pl", 0, nw)))
        if t == 0:
            masks2()
        h = lw // 2 + 16

        def valid(b, i, c0, c1):
            nm = "gr%d" % i
            tt(A(nm, 16 * c0, 16 * c1), ind(A("brow", 0, 3072), A(li, i * lw + c0, i * lw + c1)), A("mex", 16 * c0, 16 * c1), OP.is_equal)
            conv(b, [(i * lw + c0, i * lw + c1, 1, "MD", rS(nm, 16 * c0, 16 * c1))])
        b, bl, b1 = wb(), wb(), wb()
        valid(b, 1, 32, lw)
        for i, nm in ((1, "rrow"), (0, "lrow")):
            ts(A("ls16", 512 * i, 512 * i + 512), ind(A(nm, 0, P), A("snl%d" % t, 0, 32)), -1536, OP.add)
            conv(bl, [(32 * i, 32 * i + 32, 1, "MD", rS("ls16", 512 * i, 512 * i + 512))])
        valid(b, 0, 32, h)
        for k in (1, 0):
            ts(A(li, k * lw, k * lw + 32), A(bl, 32 * k, 32 * k + 32), 1536, OP.add)
            ts(A(st, k * lw, k * lw + 32), A(bl, 32 * k, 32 * k + 32), 1536, OP.add)
        ts(A("ixa", 0, 2 * lw), A(st, 0, 2 * lw), GH, OP.is_ge, -3072, OP.mult)
        tt(A("ixb", 0, 2 * lw), A("ixa", 0, 2 * lw), A(st, 0, 2 * lw), OP.add)
        ts(A("ixa", 0, 2 * lw), A("ixb", 0, 2 * lw), OWN, OP.add)
        valid(b, 1, 0, 32)
        valid(b, 0, 0, 32)
        valid(b1, 0, h, lw)
        legs(b, lw, 2 * lw)
        legs(b, 0, h)
        legs(b1, h, lw)

    def ghost_bases():
        for s in range(2):
            recv(s, "b", "gbo", 16 * s, 16 * s + 16)
        for s in range(2):
            act(A("brow", GH + 256 * s, GH + 256 * s + 256),
                ind(A("snt", 272 * s, 272 * s + 272), A("gbo", 16 * s, 16 * s + 16)))

    def legs(b, lo, hi):
        tt(A("ulf", lo, hi), A(b, lo, hi), A("ixa", lo, hi), OP.mult)
        cp(A("ul", lo, hi), A("ulf", lo, hi))

    held = {}

    def turn(t):
        P, nw = PP[t], NW[t]
        b = wb()
        conv(b, [(0, nw, 1, "MDf", rS("fr", 0, P))])
        held["b"] = b

    def pairs(t):
        nw, lw = NW[t], LW[t]
        st, B0 = "st%d" % t, 2 * LW[t]
        b = held["b"]
        ts(A("mB", 0, nw), A(st, B0, B0 + nw), GH, OP.is_lt, -88, OP.mult)
        tt(A("mB2", 0, nw), A("meS", 0, nw), A(st, B0, B0 + nw), OP.is_lt)
        tt(A("pe", 0, nw), A(b, 0, nw), A("meS", 0, nw), OP.is_equal)
        tt(A("mB2", 0, nw), A("mB2", 0, nw), A("mB", 0, nw), OP.mult)
        tt(A("mB", 0, nw), A("mB2", 0, nw), A("pe", 0, nw), OP.mult)
        ts(A("thr", 0, nw), A("mB", 0, nw), 99, OP.add)

    def flags_row(t, i):
        P, nw, lw = PP[t], NW[t], LW[t]
        o = i * lw + (32 if i < 2 else 0)
        act(A("fr", 0, P), ind(A("rrow", 0, 3072), A("li%d" % t, o, o + nw)))
        turn(t)

    def flags_col(t, i):
        nw, lw = NW[t], LW[t]
        o = i * lw + (32 if i < 2 else 0)
        b = held["b"]
        tt(A("fl", nw * i, nw * i + nw), A(b, 0, nw), A("meS", 0, nw), OP.is_equal)
        ts(A("pm2", nw * i, nw * i + nw), A("st%d" % t, o, o + nw), -GH, OP.add)

    def flags_list(t):
        nw, lw = NW[t], LW[t]
        tt(A("lff", 0, 3 * nw), A("fl", 0, 3 * nw), A("pm2", 0, 3 * nw), OP.mult)
        ts(A("lf", 0, 3 * nw), A("lff", 0, 3 * nw), GH, OP.add)
        if t == 0:
            tt(A("sna", 0, 32), A("st0", lw, lw + 32), A("slotc", 0, 32), OP.is_equal)
            ts(A("snb", 0, 32), A("sn0", 0, 32), -GH, OP.add)
            tt(A("snc", 0, 32), A("sna", 0, 32), A("snb", 0, 32), OP.mult)
            ts(A("snf", 0, 32), A("snc", 0, 32), GH, OP.add)

    def marks(u, lo, P, n):
        nm = "in%d" % (n % 2)
        for i in range(P // 512):
            ts(A(nm, 512 * i, 512 * i + 512), A(u, lo + 512 * i, lo + 512 * i + 512), A("thf", 0, 1), OP.is_ge)
            mm("p%d" % i, [(A("p%d" % i, 0, 512), A("eye", 0, 128), A(nm, 512 * i, 512 * i + 512), n == 0, n == 5)])

    def depths(t, slack):
        P, nw, lw = PP[t], NW[t], LW[t]
        for n in range(5):
            u = "U%d" % n
            gr = "gr%d" % (n % 2)
            win = A(u, 0, OWN + P)
            marks(u, OWN, P, n)
            for s in range(2):
                recv(s, str(n), u, 16 + 256 * s, 16 + 256 * s + 256)
            if n < 4:
                for s in order:
                    c = lw + 16 * s
                    act(A(gr, 256 * s, 256 * s + 256), ind(win, A("ul", c, c + 16)))
                for s in order:
                    o = A("sb%d" % (n + 1), 256 * s, 256 * s + 256)
                    tt(o, ind(win, A("ul", 16 * s, 16 * s + 16)), A(gr, 256 * s, 256 * s + 256), OP.max)
                    send(s, str(n + 1), o, "U%d" % (n + 1), 16 + 256 * (1 - s), 16 + 256 * (1 - s) + 256)
            H = P // 2
            h16 = H // 16
            for h in range(2):
                c = lw + 32 + h16 * h
                act(A(gr, 512 + H * h, 512 + H * h + H), ind(win, A("ul", c, c + h16)))
            for h in range(2):
                o = A("U%d" % (n + 1), OWN + H * h, OWN + H * h + H) if n < 4 else A("u5", H * h, H * h + H)
                c = 32 + h16 * h
                tt(o, ind(win, A("ul", c, c + h16)), A(gr, 512 + H * h, 512 + H * h + H), OP.max)
            for f in slack.get(n, []):
                f()
        marks("u5", 0, P, 5)

    def splits(t):
        P, nw, nb = PP[t], NW[t], PP[t]
        for k in range(2):
            for i in range(P // 512):
                o, x = A("in%d" % k, 512 * i, 512 * i + 512), A("p%d" % i, 0, 512)
                if (i + k) % 2 == 0:
                    act(o, x, AF.Sign)
                else:
                    ts(o, x, 0, OP.is_gt)
        b = wb()
        for c0, c1 in ((0, nw // 2), (nw // 2, nw)):
            tt(A("gr1", 16 * c0, 16 * c1), ind(A("in0", 0, P), A("pl", c0, c1)), A("in1", 16 * c0, 16 * c1), OP.max)
            conv(b, [(c0, c1, 1, "CQ", rS("gr1", 16 * c0, 16 * c1))])
        tt(A("go", 0, nw), A(b, 0, nw), A("thr", 0, nw), OP.is_ge)
        b = wb()
        mm(b, [(A(b, nw, 2 * nw), A("blk", 0, 128), A("go", 0, nw), True, True),
               (A(b, 0, nw), A("ltg", 0, 128), A("go", 0, nw), True, False),
               (A(b, 0, nw), A("eye", 0, 128), A("me16", 0, nw), False, True)])
        op("V", [lambda: g.vector.tensor_tensor_scan(X("sc", 0, nw), X(b, nw, 2 * nw), X("zer", 0, nw), 2048.0, OP.add, OP.add)],
           [(b, 0, 512), ("zer", 0, nw)], [("sc", 0, nw)])
        tt(A("ka", 0, nw), A("sc", 0, nw), A(b, 0, nw), OP.add)
        tt(A("kc", 0, nw), A("ka", 0, nw), A("go", 0, nw), OP.mult)
        tt(A("kd", 0, nw), A("kc", 0, nw), A("meS", 0, nw), OP.add)
        cp(A("koff", 0, nw), A("kd", 0, nw))
        scat(A("lrow", 0, 3072), A("koff", 0, nw), A("mex", 512, 512 + P))
        ts((X("T16", 0, 512, 2), [("T16", 0, 512)]), A("lrow", 2048, 2304), -1536, OP.add)
        b = wb()
        conv(b, [(0, 16, 1, "MD", lambda q: (X("T16", 2 * q, 512, 32), [("T16", 0, 512)]))])
        ts(A("tl", 0, 16), A(b, 0, 16), 1536, OP.add)
        ts((X("T16", 1, 512, 2), [("T16", 0, 512)]), ind(A("brow", 0, nb + 512), A("tl", 0, 16)), -1536, OP.add)
        b = wb()
        conv(b, [(0, 32, 1, "MD", rS("T16", 0, 512))])
        ts(A("TL", 0, 32), A(b, 0, 32), 1536, OP.add)
        act(A("t32", 0, 32), A(b, 0, 32), AF.Identity, bias=1536.0)

    def renames(t):
        P, nw, nb = PP[t], NW[t], PP[t]
        scat(A("NT", 0, nb + 512), A("TL", 0, 32), A("jrow", 0, 512))
        act(A("eT", 0, 512), ind(A("U0", OWN, OWN + nb + 512), A("TL", 0, 32)))
        win = A("NT", 0, 2576)
        H = P // 2
        act(A("vR", 0, P), ind(win, A("lf", nw, 2 * nw)))
        act(A("vL", H, P), ind(win, A("lf", nw // 2, nw)))
        act(A("e2", 0, 512), A("eT", 0, 512), AF.Identity, bias=128.75, scale=0.5)
        act(A("e2b", 0, 512), A("e2", 0, 512), AF.Identity, bias=-258.0)
        act(A("vy", 0, 512), ind(A("vR", 0, nb + 512), A("TL", 0, 32)))
        cp(A("vB", 0, P), ind(win, A("lf", 2 * nw, 3 * nw)))
        cp(A("vL", 0, H), ind(win, A("lf", 0, nw // 2)))
        if t == 0:
            cp(A("vs", 0, 512), ind(win, A("snf", 0, 32)))
        ts(A("Y16", 0, 512), ind(A("rrow", 0, nb + 512), A("TL", 0, 32)), -1536, OP.add)

    def update(t, lay):
        P, nw, nb = PP[t], NW[t], PP[t]
        k0 = nb - 1.5
        if lay == "S":
            a, c, ic = "st%d" % t, "st%d" % (t + 1), LW[t + 1]
            src = (32, LW[t] + 32, 2 * LW[t])
            dst = (32, ic + 32, 2 * ic)
        else:
            a, c, ic = "ns%d" % t, "ns%d" % (t + 1), nw + 32
            src = (0, nw, 2 * nw)
            dst = (0, ic, 2 * ic)

        def places(n, lo):
            if lay == "S":
                return [(lo, lo + nw, 1, "MD", rS(n, 0, P))]
            r = [(lo, lo + 96, 1, "MD", lambda q: (X(n, 96 * q, 96 * q + 96), [(n, 0, P)]))]
            if P > V0:
                r.append((lo + 96, lo + 128, 1, "MD", lambda q: (X(n, V0 + 32 * q, V0 + 32 * q + 32), [(n, 0, P)])))
            return r

        def new(n, lo, swap):
            if lay == "S":
                return [(lo, lo + 32, 1, "MD", lambda q: (X(n, q ^ swap, 512, 16), [(n, 0, 512)]))]
            if not swap:
                return [(lo, lo + 32, 1, "MD", lambda q: (X(n, 32 * q, 32 * q + 32), [(n, 0, 512)]))]
            return [(lo + e, lo + 32, 2, "MD", lambda q, e=e: (X(n, 32 * q + 1 - e, 32 * q + 32, 2), [(n, 0, 512)])) for e in range(2)]
        for i in range(3):
            act(A("pt", nw * i, nw * i + nw), A(a, src[i], src[i] + nw), AF.Identity, bias=-k0)
        b = wb()
        for n, lo in (("NT", 3 * nw), ("vB", 2 * nw), ("vR", nw), ("vL", 0)):
            conv(b, places(n, lo))
        b3, b2 = wb(), wb()
        conv(b2, new("T16", 0, 0) + new("T16", 32, 1) + new("Y16", 64, 0) + new("vy", 96, 0))
        yield
        act(A(b3, 0, 4 * nw), A(b, 0, 4 * nw), AF.Abs, bias=cb[0], scale=2.0)
        ts(A("z", 0, 4 * nw), A(b, 0, 4 * nw), 0, OP.is_equal, -8192, OP.mult)
        tt(A("q3", 0, 3 * nw), A(b3, 0, 3 * nw), A("z", 0, 3 * nw), OP.add)
        ts(A("ysn", 0, nw), A(b3, 3 * nw, 4 * nw), k0, OP.add)
        act(A(b3, 0, nw), A(b, 3 * nw, 4 * nw), AF.Abs, bias=cb[1], scale=2.0)
        tt(A("q3", 0, 3 * nw), A("q3", 0, 3 * nw), A("pt", 0, 3 * nw), OP.max)
        ts(A("q3u", 0, 3 * nw), A("q3", 0, 3 * nw), k0, OP.add)
        yield
        ts(A("sp", 0, nw), A("z", 3 * nw, 4 * nw), 0, OP.is_equal)
        ts(A("nsp", 0, nw), A("z", 3 * nw, 4 * nw), 0, OP.is_lt)
        ts(A("ysn", nw, 2 * nw), A(b3, 0, nw), k0, OP.add)
        for i in range(2):
            tt(A("yss", nw * i, nw * i + nw), A("ysn", nw * i, nw * i + nw), A("sp", 0, nw), OP.mult)
        tt(A("oc", 0, nw), A("q3u", 2 * nw, 3 * nw), A("nsp", 0, nw), OP.mult)
        tt(A("od", 0, nw), A("q3u", 0, nw), A("sp", 0, nw), OP.mult)
        tt(A(c, dst[2], dst[2] + nw), A("oc", 0, nw), A("od", 0, nw), OP.add)
        o = nw
        act(A(b3, 256, 288), A(b2, 96, 128), AF.Abs, bias=cb[0], scale=2.0)
        act(A("yt", 0, 32), A(b2, 64, 96), AF.Identity, bias=1536 - k0)
        act(A(c, dst[1] + o, dst[1] + o + 32), A(b2, 0, 32), AF.Identity, bias=1536.0)
        act(A("tsw", 0, 32), A(b2, 32, 64), AF.Identity, bias=1536.0)
        ts(A("zy", 0, 32), A(b2, 96, 128), 0, OP.is_equal, -8192, OP.mult)
        tt(A("yzy", 0, 32), A(b3, 256, 288), A("zy", 0, 32), OP.add)
        tt(A("td", 0, 32), A("yzy", 0, 32), A("yt", 0, 32), OP.max)
        ts(A(c, dst[2] + o, dst[2] + o + 32), A("td", 0, 32), k0, OP.add)
        yield
        tt(A("oa", 0, nw), A("q3u", 0, nw), A("nsp", 0, nw), OP.mult)
        tt(A(c, dst[0], dst[0] + nw), A("oa", 0, nw), A("yss", 0, nw), OP.add)
        tt(A("ob", 0, nw), A("q3u", nw, 2 * nw), A("nsp", 0, nw), OP.mult)
        tt(A(c, dst[1], dst[1] + nw), A("ob", 0, nw), A("yss", nw, 2 * nw), OP.add)
        tr = A(c, dst[1] + o, dst[1] + o + 32)
        ts(A("tab", 0, 32), tr, nb, OP.is_ge)
        tt(A("td", 0, 32), tr, A("tsw", 0, 32), OP.subtract)
        tt(A("yu", 0, 32), A("td", 0, 32), A("tab", 0, 32), OP.mult)
        tt(A(c, dst[0] + o, dst[0] + o + 32), A("tsw", 0, 32), A("yu", 0, 32), OP.add)
        yield

    def srow(x, lo, ncol, row, both):
        for i in range(ncol // 32):
            b = wb()
            mm(b, [(A(b, q, 512, 16), A("EQ", 128 * q, 128 * q + 128), A(x, lo + 32 * i, lo + 32 * i + 32), True, True) for q in range(16)])
            o = A(row, 512 * i, 512 * i + 512)
            if both and i % 2:
                ts(o, A(b, 0, 512), 1536, OP.add)
            else:
                act(o, A(b, 0, 512), AF.Identity, bias=1536.0)

    def new_snd():
        b = wb()
        conv(b, [(0, 32, 1, "MD", rS("vs", 0, 512))])
        act(A("sna", 0, 32), A(b, 0, 32), AF.Abs, bias=cb[0], scale=2.0)
        ts(A("snv", 0, 32), A(b, 0, 32), 0, OP.is_equal, -8192, OP.mult)
        tt(A("snb", 0, 32), A("sna", 0, 32), A("snv", 0, 32), OP.add)
        ts(A("snc", 0, 32), A("snb", 0, 32), V0 - 1.5, OP.add)
        tt(A("sn1", 0, 32), A("snc", 0, 32), A("sn0", 0, 32), OP.max)
        cp(A("snl1", 0, 32), A("sn1", 0, 32))
        ts(A("sn16", 0, 32), A("sn1", 0, 32), -1536, OP.add)

    def weigh(t):
        nb = PP[t]
        b = wb()
        conv(b, [(0, 32, 1, "WQ", rS("eT", 0, 512))])
        tt(A("hz", 0, 32), A(b, 0, 32), A("t32", 0, 32), OP.add)
        tt(A("hz", 32, 64), A(b, 0, 32), A("meS", nb // 16, nb // 16 + 32), OP.add)

    def children(t):
        nb = PP[t]
        ts(A("hz2", 0, 64), A("hz", 0, 64), 2047, OP.bitwise_and)
        ts(A("hq", 0, 64), A("hz2", 0, 64), -2048, OP.add)
        for i in range(2):
            ts(A("pres", 32 * i, 32 * i + 32), A("t32", 0, 32), nb, OP.is_lt)
        tt(A("hm", 0, 64), A("hq", 0, 64), A("pres", 0, 64), OP.mult)
        ts(A("eo", 0, 64), A("hm", 0, 64), 2048, OP.add)
        tt(A("cT", 0, 512), ind(A("dtb", 0, 2064), A("eo", 0, 32)), A("e2b", 0, 512), OP.add)
        scat(A("U0", OWN, OWN + nb + 512), A("TL", 0, 32), A("cT", 0, 512))
        tt(A("U0", OWN + nb, OWN + nb + 512), ind(A("dtb", 0, 2064), A("eo", 32, 64)), A("e2b", 0, 512), OP.add)

    ms(A("rrow", GH, 3088), -1.0)
    iota(A("rrow", V0, GH), [[1, 1024]], V0, 0)
    iota(A("jq", 0, 256), [[1, 256]], 1, 0)
    sel(A("tri", 0, 128), A("blk", 0, 128), [[-1, 128]], OP.is_ge, 0, 1)
    iota(A("U0", OWN + V0, OWN + GH), [[0, 1024]], 0, 0)

    def sentinels(t):
        iota(A("lrow", 2048, 2304), [[2, 256]], PP[t], 0)

    def late0():
        for q in range(16):
            act(A("MDf", 128 * q, 128 * q + 128), A("eye", 0, 128), AF.Copy, scale=A("pq", q, q + 1))
        ts(A("ltg", 0, 128), A("tri", 0, 128), -1, OP.mult)
        ts(A("me16", 0, 128), A("meS", 0, 128), -1, OP.mult)
        ms(A("zer", 0, 128), 0.0)
        cp((X("jrow", 0, 512, 2), [("jrow", 0, 512)]), A("jq", 0, 256))
        ts((X("jrow", 1, 512, 2), [("jrow", 0, 512)]), A("jq", 0, 256), -1, OP.mult)

    def masks2():
        for i in range(4):
            b = wb()
            mm(b, [(A(b, 0, 512), A("blk", 0, 128), A("MD", 512 * i, 512 * i + 512), True, True)])
            act(A("CQ", 512 * i, 512 * i + 512), A(b, 0, 512))
            act(A("WQ", 512 * i, 512 * i + 512), A(b, 0, 512), AF.Copy, scale=A("wtf", 0, 1))

    def late1():
        act(A("dtb", 0, 2048), A("dtb", 0, 2048), AF.Identity, bias=128.75, scale=0.5)
        ms(A("dtb", 2048, 2064), 129.0)
        cp(A("ns0", 0, 288), A("nraw", 0, 288))

    def late2(t):
        iota(A("NT", 0, 2576), [[0, 2576]], 0, 0)
        iota(A("vR", PP[t], PP[t] + 512), [[0, 512]], 0, 0)

    ghost_bases()
    prep(0)
    depths(0, {0: [late0, lambda: turn(0), lambda: sentinels(0)], 1: [lambda: pairs(0), lambda: flags_row(0, 0)],
               2: [lambda: flags_col(0, 0), lambda: flags_row(0, 1)],
               3: [lambda: flags_col(0, 1), lambda: flags_row(0, 2), lambda: late2(0)],
               4: [late1, lambda: flags_col(0, 2), lambda: flags_list(0)]})
    splits(0)
    renames(0)
    for _ in update(0, "S"):
        pass
    new_snd()
    lw, nw = LW[1], NW[1]
    ts(A("x16", 256, 384), A("st1", 2 * lw, 2 * lw + nw), -1536, OP.add)
    srow("x16", 256, 128, "brow", True)
    srow("sn16", 0, 32, "mex", False)
    sndtab()
    base_send(1, 2048)
    for i in (1, 0):
        ts(A("x16", 128 * i, 128 * i + 128), A("st1", lw * i + 32, lw * i + 32 + nw), -1536, OP.add)
    weigh(0)
    srow("x16", 128, 128, "rrow", False)
    ghost_bases()
    srow("x16", 0, 128, "lrow", False)
    children(0)
    ghost0(1, 2048)
    for i in range(3):
        o = lw * i + (32 if i < 2 else 0)
        cp(A("li1", o, o + nw), A("st1", o, o + nw))
    prep(1)
    un = update(0, "N")
    next(un)
    depths(1, {0: [lambda: turn(1), lambda: sentinels(1), lambda: next(un)], 1: [lambda: pairs(1), lambda: flags_row(1, 0)],
               2: [lambda: flags_col(1, 0), lambda: next(un), lambda: flags_row(1, 1)],
               3: [lambda: flags_col(1, 1), lambda: next(un), lambda: flags_row(1, 2), lambda: late2(1)],
               4: [lambda: flags_col(1, 2), lambda: flags_list(1)]})
    splits(1)
    renames(1)
    weigh(1)
    children(1)
    dma("Y", (HB("ye"), []), A("U0", OWN, OWN + GH))
    for _ in update(1, "N"):
        pass
    for i, n in ((2, "yb"), (0, "yl"), (1, "yr")):
        for j, (lo, hi, c0, c1) in enumerate(((0, 1536, 0, 96), (1536, 2048, 96, 128), (2048, 2560, 128, 160))):
            dma("SYS"[j], (T[n][:, lo:hi], []), A("ns2", 160 * i + c0, 160 * i + c1))
    wait_for("Y", {s: v for s, v in cnt.items()})
